import numpy as np
import ml_dtypes


def mxq(x, axis, fmt="e4m3"):
    dtype, down = {"e4m3": (ml_dtypes.float8_e4m3fn, 7), "e5m2": (ml_dtypes.float8_e5m2, 14)}[fmt]
    v = np.moveaxis(np.asarray(x, np.float32).astype(ml_dtypes.bfloat16).astype(np.float64), axis, -1)
    blocks = v.reshape(v.shape[:-1] + (-1, 32))
    amax = np.abs(blocks).max(-1, keepdims=True)
    byte = np.maximum(np.where(amax > 0, np.frexp(amax)[1] - 1 + 127, 0) - down, 1)
    scale = np.exp2(byte - 127.0)
    codes = (blocks / scale).astype(np.float32).astype(dtype).astype(np.float64)
    return np.moveaxis((codes * scale).reshape(v.shape), -1, axis)


WIDE = False


def mx_kscale(k):
    if not WIDE:
        return np.ones(k)
    levels = np.array([10, -10, 5, -5, 0])
    if k % 512:
        return np.exp2(np.random.permutation(np.resize(levels, k // 32))).repeat(32)
    a = np.empty((k // 512, 16))
    for p in range(k // 512):
        a[p, :8] = np.random.permutation(np.resize(levels, 8))
        for g in range(8):
            far = levels[np.abs(levels - a[p, g]) >= 10]
            a[p, g + 8] = far[np.random.randint(len(far))]
    return np.exp2(a.ravel()).repeat(32)


def f64(x):
    return np.asarray(x).astype(np.float64)


def striped(idx):
    return np.tile(idx.reshape(-1, 16).T, (8, 1)).astype(np.uint16)


def unstriped(offs):
    return offs[:16].T.reshape(-1).astype(np.int64)


def striped8(idx):
    return np.concatenate([x.reshape(-1, 16).T for x in idx]).astype(np.uint16)


def runs(offs, k):
    lists = np.stack([offs[16 * r : 16 * r + 16].T.reshape(-1) for r in range(8)]).astype(np.int64)
    return lists[np.arange(k) % 512 // 64]


def pack_weight(w):
    k, n = w.shape
    w = f64(np.asarray(w, np.float32).astype(ml_dtypes.bfloat16)).reshape(k // 32, 32, n)
    amax = np.abs(w).max(1)
    byte = np.clip(np.where(amax > 0, np.frexp(amax)[1] - 1 + 127 - 7, 1), 1, 254)
    scaled = (w * np.exp2(127.0 - byte)[:, None, :]).reshape(k, n).astype(np.float32)
    words = np.ascontiguousarray(scaled.reshape(k // 512, 128, 4, n).transpose(0, 1, 3, 2)).astype(ml_dtypes.float8_e4m3fn).view(np.uint8)
    return words, np.ascontiguousarray(byte.astype(np.uint8).reshape(k // 512, 16, n))


def unpack_weight(words, scales):
    g, p, n, _ = words.shape
    vals = np.ascontiguousarray(words).view(ml_dtypes.float8_e4m3fn).astype(np.float64) * np.repeat(np.exp2(scales.astype(np.float64) - 127.0), 8, axis=1)[..., None]
    return vals.transpose(0, 1, 3, 2).reshape(g * 512, n)


def relu(v):
    return np.maximum(v, 0.0)


K, T, S, V, N, H = 512, 2048, 1024, 512, 512, 512


def setup_inputs():
    n = np.random.standard_normal
    s = mx_kscale(K)[:, None]
    u = mx_kscale(H)
    packed_xT = pack_weight(n((K, T)) * s)
    return {
        "x_words": packed_xT[0],
        "x_scales": packed_xT[1],
        "w1": (n((K, H)) / np.sqrt(K) / s * u).astype(np.float32),
        "w2": (n((H, N)) / np.sqrt(H) / u[:, None]).astype(np.float32),
        "offs": striped(np.random.permutation(T)[:S]),
        "order": striped8(np.stack([np.random.permutation(S) for _ in range(8)])),
        "bucket": striped8(np.random.randint(0, V, (8, S))),
    }


def reference(x_words, x_scales, w1, w2, offs, order, bucket):
    xq = unpack_weight(x_words, x_scales)[:, unstriped(offs)]
    y = mxq(f64(w1), 0, "e4m3").T @ xq
    s = y[np.arange(H)[:, None], runs(order, H)]
    p = s.reshape(H, V, 2).mean(axis=2)
    z = relu(y - (p[np.arange(H)[:, None], runs(bucket, H)]))
    return mxq(f64(w2), 0, "e4m3").T @ mxq(z, 0, "e4m3")

@@ -1,0 +1,165 @@
+from contextlib import ExitStack
+
+import concourse.mybir as mybir
+
+K, T, S, V, N, H = 512, 2048, 1024, 512, 512, 512
+FLOPS = 2 * K * H * S + 2 * H * N * S
+
+F32 = mybir.dt.float32
+BF16 = mybir.dt.bfloat16
+I32 = mybir.dt.int32
+U32 = mybir.dt.uint32
+U16 = mybir.dt.uint16
+U8 = mybir.dt.uint8
+FP8X4 = mybir.dt.float8_e4m3fn_x4
+ALU = mybir.AluOpType
+ACT = mybir.ActivationFunctionType
+
+P = 128
+PACK = 4
+HALF = 512
+CHUNKS = (128, 256, 256, 256, 128)
+
+
+def tile_picked_lshmean_relu_p_kernel(tc, x_words, x_scales, w1, w2, offs, order, bucket, out):
+    nc = tc.nc
+    with ExitStack() as ctx:
+        keep = ctx.enter_context(tc.tile_pool(name="keep", bufs=1))
+        ring = ctx.enter_context(tc.tile_pool(name="ring", bufs=2))
+        psum = ctx.enter_context(tc.psum_pool(name="psum", bufs=4))
+
+        offs_sb = keep.tile([P, S // 16], U16, name="offs_sb")
+        order_sb = keep.tile([P, S // 16], U16, name="order_sb")
+        bucket_sb = keep.tile([P, S // 16], U16, name="bucket_sb")
+        words_all = keep.tile([P, T], U32, name="words_all", align_bytes=64)
+        scales_all = keep.tile([P, T], U8, name="scales_all", align_bytes=64)
+        w1_raw = keep.tile([P, PACK, H], F32, name="w1_raw", align_bytes=64)
+
+        nc.vector.memset(scales_all[:].bitcast(I32), 0)
+        nc.sync.dma_start(offs_sb[:], offs)
+        nc.sync.dma_start(order_sb[:], order)
+        nc.sync.dma_start(bucket_sb[:], bucket)
+        for q in range(4):
+            nc.sync.dma_start(out=scales_all[32 * q : 32 * q + 4, :].bitcast(I32), in_=x_scales[0, 4 * q : 4 * q + 4, :].bitcast(I32))
+        nc.sync.dma_start(out=words_all[:].bitcast(I32), in_=x_words[0].rearrange("p n r -> p (n r)").bitcast(I32))
+        nc.sync.dma_start(out=w1_raw[:], in_=w1.rearrange("(p j) h -> p j h", j=PACK))
+        w2_all = keep.tile([P, PACK, N], F32, name="w2_all", align_bytes=64)
+        w2_view = w2.rearrange("(b t i) m -> t b i m", t=PACK, i=8)
+        for t in range(PACK):
+            nc.sync.dma_start(out=w2_all[:, t, :], in_=w2_view[t])
+
+        x_sc = keep.tile([P, S], U8, name="x_sc", align_bytes=64)
+        nc.vector.tensor_copy(x_sc[:], scales_all[:].indirect(offs_sb[:]))
+        x_cd = [keep.tile([P, HALF], U32, name=f"x_cd{h}", align_bytes=64) for h in range(2)]
+        for h in range(2):
+            nc.vector.tensor_copy(x_cd[h][:], words_all[:].indirect(offs_sb[:, 32 * h : 32 * h + 32]))
+
+        w1_view = w1_raw[:].rearrange("p j (b t i) -> p t b i j", t=PACK, i=8)
+        w1_cd, w1_sc = [], []
+
+        def cast_w1(t):
+            g = keep.tile([P, P * PACK], BF16, name=f"w1_g{t}", align_bytes=64)
+            dst = g[:].rearrange("p (b i j) -> p b i j", i=8, j=PACK)
+            nc.scalar.copy(out=dst, in_=w1_view[:, t])
+            return g
+
+        def quant_w1(t, g):
+            cd = keep.tile([P, P], U32, name=f"w1_cd{t}", align_bytes=64)
+            sc = keep.tile([P, P], U8, name=f"w1_sc{t}", align_bytes=64)
+            nc.vector.quantize_mx(out=cd[:].bitcast(FP8X4), scales=sc[:], in_=g[:])
+            w1_cd.append(cd)
+            w1_sc.append(sc)
+
+        y = [keep.tile([P, S], F32, name=f"y{t}", align_bytes=64) for t in range(PACK)]
+
+        def first_product(t):
+            n = 256 if t == 0 else HALF
+            for c0 in range(0, S, n):
+                acc = psum.tile([P, n], F32, name="acc_y")
+                nc.tensor.matmul_mx(out=acc[:], lhsT=w1_cd[t][:].bitcast(FP8X4), lhsT_scale=w1_sc[t][:],
+                                    rhs=x_cd[c0 // HALF][:, c0 % HALF : c0 % HALF + n].bitcast(FP8X4), rhs_scale=x_sc[:, c0 : c0 + n], start=True, stop=True)
+                if t == 0:
+                    nc.vector.tensor_copy(out=y[t][:, c0 : c0 + n], in_=acc[:])
+                else:
+                    nc.scalar.copy(out=y[t][:, c0 : c0 + n], in_=acc[:])
+
+        gs = [cast_w1(0), cast_w1(1)]
+        quant_w1(0, gs[0])
+        first_product(0)
+        quant_w1(1, gs[1])
+        gs.append(cast_w1(2))
+        first_product(1)
+        quant_w1(2, gs[2])
+        gs.append(cast_w1(3))
+        first_product(2)
+        quant_w1(3, gs[3])
+        first_product(3)
+
+        w2_g = keep.tile([P, N * PACK], BF16, name="w2_g", align_bytes=64)
+        nc.scalar.copy(out=w2_g[:].rearrange("p (m t) -> p m t", t=PACK), in_=w2_all[:].rearrange("p t m -> p m t"))
+
+        means = [keep.tile([P, V], F32, name=f"mean{t}", align_bytes=64) for t in range(PACK)]
+        lined = []
+
+        def pair(t):
+            pr = lined[t][:].rearrange("p (v e) -> p v e", e=2)
+            nc.vector.tensor_tensor(out=means[t][:], in0=pr[:, :, 0], in1=pr[:, :, 1], op=ALU.add)
+
+        for t in range(PACK):
+            s = ring.tile([P, S], F32, name="lined")
+            lined.append(s)
+            for h in range(2):
+                nc.vector.tensor_scalar(s[:, HALF * h : HALF * (h + 1)], y[t][:].indirect(order_sb[:, 32 * h : 32 * h + 32]),
+                                        0.5, 0.0, ALU.mult, ALU.add)
+                if h == 0 and t > 0:
+                    pair(t - 1)
+        w2_cd = keep.tile([P, N], U32, name="w2_cd", align_bytes=64)
+        w2_sc = keep.tile([P, N], U8, name="w2_sc", align_bytes=64)
+        nc.vector.quantize_mx(out=w2_cd[:].bitcast(FP8X4), scales=w2_sc[:], in_=w2_g[:])
+        pair(PACK - 1)
+
+        out_view = out.rearrange("(g p) s -> p g s", p=P)
+
+        def front(c0, n, last):
+            d = ring.tile([P, PACK, n], F32, name="diff")
+            for t in range(PACK):
+                nc.vector.tensor_tensor(d[:, t, :], means[t][:].indirect(bucket_sb[:, c0 // 16 : (c0 + n) // 16]), y[t][:, c0 : c0 + n], ALU.subtract)
+            z = ring.tile([P, n * PACK], BF16, name="z", align_bytes=64)
+            return d, z
+
+        def relu(d, z, last):
+            dst = z[:].rearrange("p (s t) -> p s t", t=PACK)
+            src = d[:].rearrange("p t s -> p s t")
+            if last:
+                nc.vector.tensor_scalar(dst, src, -1.0, 0.0, ALU.mult, ALU.max)
+            else:
+                nc.scalar.activation(out=dst, in_=src, func=ACT.Relu, scale=-1.0)
+
+        def back(c0, n, z, last):
+            z_cd = ring.tile([P, n], U32, name="z_cd", align_bytes=64)
+            z_sc = ring.tile([P, n], U8, name="z_sc", align_bytes=64)
+            nc.vector.quantize_mx(out=z_cd[:].bitcast(FP8X4), scales=z_sc[:], in_=z[:])
+            for u in range(2):
+                acc = psum.tile([P, 2, n], F32, name="acc_o")
+                for k in range(2):
+                    g = 2 * u + k
+                    nc.tensor.matmul_mx(out=acc[:, k, :], lhsT=w2_cd[:, P * g : P * (g + 1)].bitcast(FP8X4), lhsT_scale=w2_sc[:, P * g : P * (g + 1)],
+                                        rhs=z_cd[:].bitcast(FP8X4), rhs_scale=z_sc[:], start=True, stop=True)
+                res = keep.tile([P, 2, n], F32, name=f"res{c0}_{u}")
+                if last and u == 1:
+                    nc.vector.tensor_copy(out=res[:], in_=acc[:])
+                else:
+                    nc.scalar.copy(out=res[:], in_=acc[:])
+                (nc.scalar if last and u == 0 else nc.sync).dma_start(out=out_view[:, 2 * u : 2 * u + 2, c0 : c0 + n], in_=res[:])
+
+        c0 = 0
+        prev = None
+        for ci, n in enumerate(CHUNKS):
+            last = ci == len(CHUNKS) - 1
+            d, z = front(c0, n, last)
+            if prev is not None:
+                back(*prev)
+            relu(d, z, last)
+            prev = (c0, n, z, last)
+            c0 += n
+        back(*prev)

@@ -26,7 +26,7 @@ def tile_picked_lshmean_relu_p_kernel(tc, x_words, x_scales, w1, w2, offs, order
     with ExitStack() as ctx:
         keep = ctx.enter_context(tc.tile_pool(name="keep", bufs=1))
         ring = ctx.enter_context(tc.tile_pool(name="ring", bufs=2))
-        psum = ctx.enter_context(tc.psum_pool(name="psum", bufs=4))
+        psum = ctx.enter_context(tc.psum_pool(name="psum", bufs=8))
 
         offs_sb = keep.tile([P, S // 16], U16, name="offs_sb")
         order_sb = keep.tile([P, S // 16], U16, name="order_sb")
@@ -37,29 +37,28 @@ def tile_picked_lshmean_relu_p_kernel(tc, x_words, x_scales, w1, w2, offs, order
 
         nc.vector.memset(scales_all[:].bitcast(I32), 0)
         nc.sync.dma_start(offs_sb[:], offs)
+        nc.sync.dma_start(out=words_all[:].bitcast(I32), in_=x_words[0].rearrange("p n r -> p (n r)").bitcast(I32))
         nc.sync.dma_start(order_sb[:], order)
         nc.sync.dma_start(bucket_sb[:], bucket)
         for q in range(4):
             nc.sync.dma_start(out=scales_all[32 * q : 32 * q + 4, :].bitcast(I32), in_=x_scales[0, 4 * q : 4 * q + 4, :].bitcast(I32))
-        nc.sync.dma_start(out=words_all[:].bitcast(I32), in_=x_words[0].rearrange("p n r -> p (n r)").bitcast(I32))
         nc.sync.dma_start(out=w1_raw[:], in_=w1.rearrange("(p j) h -> p j h", j=PACK))
         w2_all = keep.tile([P, PACK, N], F32, name="w2_all", align_bytes=64)
         w2_view = w2.rearrange("(b t i) m -> t b i m", t=PACK, i=8)
         for t in range(PACK):
             nc.sync.dma_start(out=w2_all[:, t, :], in_=w2_view[t])
 
-        x_sc = keep.tile([P, S], U8, name="x_sc", align_bytes=64)
-        nc.vector.tensor_copy(x_sc[:], scales_all[:].indirect(offs_sb[:]))
-        x_cd = [keep.tile([P, HALF], U32, name=f"x_cd{h}", align_bytes=64) for h in range(2)]
-        for h in range(2):
-            nc.vector.tensor_copy(x_cd[h][:], words_all[:].indirect(offs_sb[:, 32 * h : 32 * h + 32]))
+        x_cd = keep.tile([P, S], U32, name="x_cd", tag="x_cd", align_bytes=64)
+        nc.vector.tensor_copy(x_cd[:], words_all[:].indirect(offs_sb[:]))
+        x_sc = [keep.tile([P, HALF], U8, name="x_sc0", align_bytes=64)]
+        nc.vector.tensor_copy(x_sc[0][:], scales_all[:].indirect(offs_sb[:, 0:32]))
 
-        w1_view = w1_raw[:].rearrange("p j (b t i) -> p t b i j", t=PACK, i=8)
+        w1_view = w1_raw[:].rearrange("p j (b t c i) -> p t b c j i", t=PACK, c=2, i=4)
         w1_cd, w1_sc = [], []
 
         def cast_w1(t):
-            g = keep.tile([P, P * PACK], BF16, name=f"w1_g{t}", align_bytes=64)
-            dst = g[:].rearrange("p (b i j) -> p b i j", i=8, j=PACK)
+            g = keep.tile([P, P * PACK], BF16, name=f"w1_g{t}", tag=f"w1_g{t}", align_bytes=64)
+            dst = g[:].rearrange("p (b c i j) -> p b c j i", c=2, i=4, j=PACK)
             nc.scalar.copy(out=dst, in_=w1_view[:, t])
             return g
 
@@ -75,16 +74,16 @@ def tile_picked_lshmean_relu_p_kernel(tc, x_words, x_scales, w1, w2, offs, order
         def first_product(t):
             n = 256 if t == 0 else HALF
             for c0 in range(0, S, n):
-                acc = psum.tile([P, n], F32, name="acc_y")
+                acc = psum.tile([P, n], F32, name="acc_y", tag="acc")
                 nc.tensor.matmul_mx(out=acc[:], lhsT=w1_cd[t][:].bitcast(FP8X4), lhsT_scale=w1_sc[t][:],
-                                    rhs=x_cd[c0 // HALF][:, c0 % HALF : c0 % HALF + n].bitcast(FP8X4), rhs_scale=x_sc[:, c0 : c0 + n], start=True, stop=True)
-                if t == 0:
-                    nc.vector.tensor_copy(out=y[t][:, c0 : c0 + n], in_=acc[:])
-                else:
-                    nc.scalar.copy(out=y[t][:, c0 : c0 + n], in_=acc[:])
+                                    rhs=x_cd[:, c0 : c0 + n].bitcast(FP8X4), rhs_scale=x_sc[c0 // HALF][:, c0 % HALF : c0 % HALF + n], start=True, stop=True)
+                nc.scalar.copy(out=y[t][:, c0 : c0 + n], in_=acc[:])
 
         gs = [cast_w1(0), cast_w1(1)]
         quant_w1(0, gs[0])
+        x_sc.append(keep.tile([P, HALF], U8, name="x_sc1", tag="w1_g0", align_bytes=64))
+        for c0 in (0, 256):
+            nc.vector.tensor_copy(x_sc[1][:, c0 : c0 + 256], scales_all[:].indirect(offs_sb[:, 32 + c0 // 16 : 48 + c0 // 16]))
         first_product(0)
         quant_w1(1, gs[1])
         gs.append(cast_w1(2))
@@ -95,41 +94,47 @@ def tile_picked_lshmean_relu_p_kernel(tc, x_words, x_scales, w1, w2, offs, order
         quant_w1(3, gs[3])
         first_product(3)
 
-        w2_g = keep.tile([P, N * PACK], BF16, name="w2_g", align_bytes=64)
-        nc.scalar.copy(out=w2_g[:].rearrange("p (m t) -> p m t", t=PACK), in_=w2_all[:].rearrange("p t m -> p m t"))
+        w2_g = keep.tile([P, N * PACK], BF16, name="w2_g", tag="x_cd", align_bytes=64)
+        nc.scalar.copy(out=w2_g[:].rearrange("p (c i t) -> p c t i", i=4, t=PACK), in_=w2_all[:].rearrange("p t (c i) -> p c t i", i=4))
 
         means = [keep.tile([P, V], F32, name=f"mean{t}", align_bytes=64) for t in range(PACK)]
         lined = []
 
         def pair(t):
             pr = lined[t][:].rearrange("p (v e) -> p v e", e=2)
-            nc.vector.tensor_tensor(out=means[t][:], in0=pr[:, :, 0], in1=pr[:, :, 1], op=ALU.add)
+            if t < PACK - 1:
+                nc.gpsimd.tensor_tensor(out=means[t][:], in0=pr[:, :, 0], in1=pr[:, :, 1], op=ALU.add)
+            else:
+                for v0 in (0, V // 2):
+                    vs = slice(v0, v0 + V // 2)
+                    nc.vector.tensor_tensor(out=means[t][:, vs], in0=pr[:, vs, 0], in1=pr[:, vs, 1], op=ALU.add)
 
         for t in range(PACK):
-            s = ring.tile([P, S], F32, name="lined")
+            s = ring.tile([P, S], F32, name="lined", tag="work")
             lined.append(s)
             for h in range(2):
                 nc.vector.tensor_scalar(s[:, HALF * h : HALF * (h + 1)], y[t][:].indirect(order_sb[:, 32 * h : 32 * h + 32]),
                                         0.5, 0.0, ALU.mult, ALU.add)
-                if h == 0 and t > 0:
-                    pair(t - 1)
+            pair(t)
         w2_cd = keep.tile([P, N], U32, name="w2_cd", align_bytes=64)
         w2_sc = keep.tile([P, N], U8, name="w2_sc", align_bytes=64)
         nc.vector.quantize_mx(out=w2_cd[:].bitcast(FP8X4), scales=w2_sc[:], in_=w2_g[:])
-        pair(PACK - 1)
 
         out_view = out.rearrange("(g p) s -> p g s", p=P)
 
         def front(c0, n, last):
-            d = ring.tile([P, PACK, n], F32, name="diff")
+            d = ring.tile([P, PACK, n], F32, name="diff", tag="work")
             for t in range(PACK):
                 nc.vector.tensor_tensor(d[:, t, :], means[t][:].indirect(bucket_sb[:, c0 // 16 : (c0 + n) // 16]), y[t][:, c0 : c0 + n], ALU.subtract)
-            z = ring.tile([P, n * PACK], BF16, name="z", align_bytes=64)
+            if c0 + n >= S - CHUNKS[-1]:
+                z = keep.tile([P, n * PACK], BF16, name="z_end", align_bytes=64)
+            else:
+                z = ring.tile([P, n * PACK], BF16, name="z", align_bytes=64)
             return d, z
 
         def relu(d, z, last):
-            dst = z[:].rearrange("p (s t) -> p s t", t=PACK)
-            src = d[:].rearrange("p t s -> p s t")
+            dst = z[:].rearrange("p (c i t) -> p c t i", i=4, t=PACK)
+            src = d[:].rearrange("p t (c i) -> p c t i", i=4)
             if last:
                 nc.vector.tensor_scalar(dst, src, -1.0, 0.0, ALU.mult, ALU.max)
             else:
@@ -140,17 +145,17 @@ def tile_picked_lshmean_relu_p_kernel(tc, x_words, x_scales, w1, w2, offs, order
             z_sc = ring.tile([P, n], U8, name="z_sc", align_bytes=64)
             nc.vector.quantize_mx(out=z_cd[:].bitcast(FP8X4), scales=z_sc[:], in_=z[:])
             for u in range(2):
-                acc = psum.tile([P, 2, n], F32, name="acc_o")
+                acc = psum.tile([P, 2, n], F32, name="acc_o", tag="acc")
                 for k in range(2):
                     g = 2 * u + k
                     nc.tensor.matmul_mx(out=acc[:, k, :], lhsT=w2_cd[:, P * g : P * (g + 1)].bitcast(FP8X4), lhsT_scale=w2_sc[:, P * g : P * (g + 1)],
                                         rhs=z_cd[:].bitcast(FP8X4), rhs_scale=z_sc[:], start=True, stop=True)
                 res = keep.tile([P, 2, n], F32, name=f"res{c0}_{u}")
-                if last and u == 1:
+                if c0 + n >= S - CHUNKS[-1] and u == 0:
                     nc.vector.tensor_copy(out=res[:], in_=acc[:])
                 else:
                     nc.scalar.copy(out=res[:], in_=acc[:])
-                (nc.scalar if last and u == 0 else nc.sync).dma_start(out=out_view[:, 2 * u : 2 * u + 2, c0 : c0 + n], in_=res[:])
+                (nc.scalar if last and u == 1 else nc.sync).dma_start(out=out_view[:, 2 * u : 2 * u + 2, c0 : c0 + n], in_=res[:])
 
         c0 = 0
         prev = None

@@ -18,7 +18,7 @@ ACT = mybir.ActivationFunctionType
 P = 128
 PACK = 4
 HALF = 512
-CHUNKS = (128, 256, 256, 256, 128)
+CHUNKS = (256, 256, 256, 128, 128)
 
 
 def tile_picked_lshmean_relu_p_kernel(tc, x_words, x_scales, w1, w2, offs, order, bucket, out):
@@ -33,34 +33,35 @@ def tile_picked_lshmean_relu_p_kernel(tc, x_words, x_scales, w1, w2, offs, order
         bucket_sb = keep.tile([P, S // 16], U16, name="bucket_sb")
         words_all = keep.tile([P, T], U32, name="words_all", align_bytes=64)
         scales_all = keep.tile([P, T], U8, name="scales_all", align_bytes=64)
-        w1_raw = keep.tile([P, PACK, H], F32, name="w1_raw", align_bytes=64)
+        w1_raw = [keep.tile([P, 2, H], F32, name=f"w1_raw{u}", align_bytes=64) for u in range(2)]
 
         nc.vector.memset(scales_all[:].bitcast(I32), 0)
         nc.sync.dma_start(offs_sb[:], offs)
-        nc.sync.dma_start(out=words_all[:].bitcast(I32), in_=x_words[0].rearrange("p n r -> p (n r)").bitcast(I32))
-        nc.sync.dma_start(order_sb[:], order)
-        nc.sync.dma_start(bucket_sb[:], bucket)
+        w1_rows = w1.rearrange("(p u j) h -> u p j h", u=2, j=2)
+        nc.sync.dma_start(out=w1_raw[0][:], in_=w1_rows[0])
         for q in range(4):
             nc.sync.dma_start(out=scales_all[32 * q : 32 * q + 4, :].bitcast(I32), in_=x_scales[0, 4 * q : 4 * q + 4, :].bitcast(I32))
-        nc.sync.dma_start(out=w1_raw[:], in_=w1.rearrange("(p j) h -> p j h", j=PACK))
+        nc.sync.dma_start(out=words_all[:].bitcast(I32), in_=x_words[0].rearrange("p n r -> p (n r)").bitcast(I32))
+        nc.sync.dma_start(out=w1_raw[1][:], in_=w1_rows[1])
+        nc.sync.dma_start(order_sb[:], order)
+        nc.sync.dma_start(bucket_sb[:], bucket)
         w2_all = keep.tile([P, PACK, N], F32, name="w2_all", align_bytes=64)
         w2_view = w2.rearrange("(b t i) m -> t b i m", t=PACK, i=8)
         for t in range(PACK):
             nc.sync.dma_start(out=w2_all[:, t, :], in_=w2_view[t])
 
-        x_cd = keep.tile([P, S], U32, name="x_cd", tag="x_cd", align_bytes=64)
-        nc.vector.tensor_copy(x_cd[:], words_all[:].indirect(offs_sb[:]))
-        x_sc = [keep.tile([P, HALF], U8, name="x_sc0", align_bytes=64)]
-        nc.vector.tensor_copy(x_sc[0][:], scales_all[:].indirect(offs_sb[:, 0:32]))
+        x_sc = keep.tile([P, S], U8, name="x_sc", align_bytes=64)
+        nc.vector.tensor_copy(x_sc[:], scales_all[:].indirect(offs_sb[:]))
+        x_cd = [keep.tile([P, 768], U32, name="x_cd0", tag="x_cd", align_bytes=64)]
+        nc.vector.tensor_copy(x_cd[0][:], words_all[:].indirect(offs_sb[:, 0:48]))
 
-        w1_view = w1_raw[:].rearrange("p j (b t c i) -> p t b c j i", t=PACK, c=2, i=4)
+        w1_view = [w1_raw[u][:].rearrange("p j (b t i) -> p t b i j", t=PACK, i=8) for u in range(2)]
+        gs = [keep.tile([P, P * PACK], BF16, name=f"w1_g{t}", tag=f"w1_g{t}", align_bytes=64) for t in range(PACK)]
         w1_cd, w1_sc = [], []
 
-        def cast_w1(t):
-            g = keep.tile([P, P * PACK], BF16, name=f"w1_g{t}", tag=f"w1_g{t}", align_bytes=64)
-            dst = g[:].rearrange("p (b c i j) -> p b c j i", c=2, i=4, j=PACK)
-            nc.scalar.copy(out=dst, in_=w1_view[:, t])
-            return g
+        def cast_w1(t, u):
+            dst = gs[t][:].rearrange("p (b i u j) -> p u b i j", i=8, u=2, j=2)
+            nc.scalar.copy(out=dst[:, u], in_=w1_view[u][:, t])
 
         def quant_w1(t, g):
             cd = keep.tile([P, P], U32, name=f"w1_cd{t}", align_bytes=64)
@@ -72,50 +73,41 @@ def tile_picked_lshmean_relu_p_kernel(tc, x_words, x_scales, w1, w2, offs, order
         y = [keep.tile([P, S], F32, name=f"y{t}", align_bytes=64) for t in range(PACK)]
 
         def first_product(t):
-            n = 256 if t == 0 else HALF
-            for c0 in range(0, S, n):
+            for c0, n in ((0, 256), (256, 256), (512, 256), (768, 256)) if t == 0 else ((0, 512), (512, 256), (768, 256)):
                 acc = psum.tile([P, n], F32, name="acc_y", tag="acc")
                 nc.tensor.matmul_mx(out=acc[:], lhsT=w1_cd[t][:].bitcast(FP8X4), lhsT_scale=w1_sc[t][:],
-                                    rhs=x_cd[:, c0 : c0 + n].bitcast(FP8X4), rhs_scale=x_sc[c0 // HALF][:, c0 % HALF : c0 % HALF + n], start=True, stop=True)
+                                    rhs=x_cd[c0 // 768][:, c0 % 768 : c0 % 768 + n].bitcast(FP8X4), rhs_scale=x_sc[:, c0 : c0 + n], start=True, stop=True)
                 nc.scalar.copy(out=y[t][:, c0 : c0 + n], in_=acc[:])
 
-        gs = [cast_w1(0), cast_w1(1)]
+        for u in range(2):
+            for t in range(PACK):
+                cast_w1(t, u)
         quant_w1(0, gs[0])
-        x_sc.append(keep.tile([P, HALF], U8, name="x_sc1", tag="w1_g0", align_bytes=64))
-        for c0 in (0, 256):
-            nc.vector.tensor_copy(x_sc[1][:, c0 : c0 + 256], scales_all[:].indirect(offs_sb[:, 32 + c0 // 16 : 48 + c0 // 16]))
-        first_product(0)
-        quant_w1(1, gs[1])
-        gs.append(cast_w1(2))
-        first_product(1)
-        quant_w1(2, gs[2])
-        gs.append(cast_w1(3))
-        first_product(2)
-        quant_w1(3, gs[3])
-        first_product(3)
+        x_cd.append(keep.tile([P, 256], U32, name="x_cd1", tag="w1_g0", align_bytes=64))
+        nc.vector.tensor_copy(x_cd[1][:], words_all[:].indirect(offs_sb[:, 48:64]))
+        for t in range(1, PACK):
+            quant_w1(t, gs[t])
+        for t in range(PACK):
+            first_product(t)
 
         w2_g = keep.tile([P, N * PACK], BF16, name="w2_g", tag="x_cd", align_bytes=64)
         nc.scalar.copy(out=w2_g[:].rearrange("p (c i t) -> p c t i", i=4, t=PACK), in_=w2_all[:].rearrange("p t (c i) -> p c t i", i=4))
 
         means = [keep.tile([P, V], F32, name=f"mean{t}", align_bytes=64) for t in range(PACK)]
-        lined = []
-
-        def pair(t):
-            pr = lined[t][:].rearrange("p (v e) -> p v e", e=2)
-            if t < PACK - 1:
-                nc.gpsimd.tensor_tensor(out=means[t][:], in0=pr[:, :, 0], in1=pr[:, :, 1], op=ALU.add)
-            else:
-                for v0 in (0, V // 2):
-                    vs = slice(v0, v0 + V // 2)
-                    nc.vector.tensor_tensor(out=means[t][:, vs], in0=pr[:, vs, 0], in1=pr[:, vs, 1], op=ALU.add)
 
         for t in range(PACK):
-            s = ring.tile([P, S], F32, name="lined", tag="work")
-            lined.append(s)
+            if t < 2:
+                s = keep.tile([P, S], F32, name=f"lined{t}")
+            else:
+                s = ring.tile([P, S], F32, name="lined", tag="work")
+            pr = s[:].rearrange("p (v e) -> p v e", e=2)
             for h in range(2):
                 nc.vector.tensor_scalar(s[:, HALF * h : HALF * (h + 1)], y[t][:].indirect(order_sb[:, 32 * h : 32 * h + 32]),
                                         0.5, 0.0, ALU.mult, ALU.add)
-            pair(t)
+            for h in range(2):
+                vs = slice(V // 2 * h, V // 2 * (h + 1))
+                eng = nc.vector if (t, h) == (PACK - 1, 1) else nc.gpsimd
+                eng.tensor_tensor(out=means[t][:, vs], in0=pr[:, vs, 0], in1=pr[:, vs, 1], op=ALU.add)
         w2_cd = keep.tile([P, N], U32, name="w2_cd", align_bytes=64)
         w2_sc = keep.tile([P, N], U8, name="w2_sc", align_bytes=64)
         nc.vector.quantize_mx(out=w2_cd[:].bitcast(FP8X4), scales=w2_sc[:], in_=w2_g[:])

@@ -77,7 +77,10 @@ def tile_picked_lshmean_relu_p_kernel(tc, x_words, x_scales, w1, w2, offs, order
                 acc = psum.tile([P, n], F32, name="acc_y", tag="acc")
                 nc.tensor.matmul_mx(out=acc[:], lhsT=w1_cd[t][:].bitcast(FP8X4), lhsT_scale=w1_sc[t][:],
                                     rhs=x_cd[c0 // 768][:, c0 % 768 : c0 % 768 + n].bitcast(FP8X4), rhs_scale=x_sc[:, c0 : c0 + n], start=True, stop=True)
-                nc.scalar.copy(out=y[t][:, c0 : c0 + n], in_=acc[:])
+                if (t, c0) == (0, HALF):
+                    nc.vector.tensor_copy(out=y[t][:, c0 : c0 + n], in_=acc[:])
+                else:
+                    nc.scalar.copy(out=y[t][:, c0 : c0 + n], in_=acc[:])
 
         for u in range(2):
             for t in range(PACK):
@@ -118,16 +121,16 @@ def tile_picked_lshmean_relu_p_kernel(tc, x_words, x_scales, w1, w2, offs, order
             d = ring.tile([P, PACK, n], F32, name="diff", tag="work")
             for t in range(PACK):
                 nc.vector.tensor_tensor(d[:, t, :], means[t][:].indirect(bucket_sb[:, c0 // 16 : (c0 + n) // 16]), y[t][:, c0 : c0 + n], ALU.subtract)
-            if c0 + n >= S - CHUNKS[-1]:
+            if c0 >= HALF:
                 z = keep.tile([P, n * PACK], BF16, name="z_end", align_bytes=64)
             else:
                 z = ring.tile([P, n * PACK], BF16, name="z", align_bytes=64)
             return d, z
 
-        def relu(d, z, last):
+        def relu(d, z, small):
             dst = z[:].rearrange("p (c i t) -> p c t i", i=4, t=PACK)
             src = d[:].rearrange("p t (c i) -> p c t i", i=4)
-            if last:
+            if small:
                 nc.vector.tensor_scalar(dst, src, -1.0, 0.0, ALU.mult, ALU.max)
             else:
                 nc.scalar.activation(out=dst, in_=src, func=ACT.Relu, scale=-1.0)
@@ -136,18 +139,19 @@ def tile_picked_lshmean_relu_p_kernel(tc, x_words, x_scales, w1, w2, offs, order
             z_cd = ring.tile([P, n], U32, name="z_cd", align_bytes=64)
             z_sc = ring.tile([P, n], U8, name="z_sc", align_bytes=64)
             nc.vector.quantize_mx(out=z_cd[:].bitcast(FP8X4), scales=z_sc[:], in_=z[:])
-            for u in range(2):
-                acc = psum.tile([P, 2, n], F32, name="acc_o", tag="acc")
-                for k in range(2):
-                    g = 2 * u + k
+            per = 1 if last else 2
+            for u in range(PACK // per):
+                acc = psum.tile([P, per, n], F32, name="acc_o", tag="acc")
+                for k in range(per):
+                    g = per * u + k
                     nc.tensor.matmul_mx(out=acc[:, k, :], lhsT=w2_cd[:, P * g : P * (g + 1)].bitcast(FP8X4), lhsT_scale=w2_sc[:, P * g : P * (g + 1)],
                                         rhs=z_cd[:].bitcast(FP8X4), rhs_scale=z_sc[:], start=True, stop=True)
-                res = keep.tile([P, 2, n], F32, name=f"res{c0}_{u}")
-                if c0 + n >= S - CHUNKS[-1] and u == 0:
+                res = keep.tile([P, per, n], F32, name=f"res{c0}_{u}")
+                if last and u % 2 == 0:
                     nc.vector.tensor_copy(out=res[:], in_=acc[:])
                 else:
                     nc.scalar.copy(out=res[:], in_=acc[:])
-                (nc.scalar if last and u == 1 else nc.sync).dma_start(out=out_view[:, 2 * u : 2 * u + 2, c0 : c0 + n], in_=res[:])
+                (nc.scalar if last and u % 2 == 1 else nc.sync).dma_start(out=out_view[:, per * u : per * (u + 1), c0 : c0 + n], in_=res[:])
 
         c0 = 0
         prev = None
@@ -156,7 +160,7 @@ def tile_picked_lshmean_relu_p_kernel(tc, x_words, x_scales, w1, w2, offs, order
             d, z = front(c0, n, last)
             if prev is not None:
                 back(*prev)
-            relu(d, z, last)
+            relu(d, z, n == 128)
             prev = (c0, n, z, last)
             c0 += n
         back(*prev)

@@ -33,14 +33,14 @@ def tile_picked_lshmean_relu_p_kernel(tc, x_words, x_scales, w1, w2, offs, order
         bucket_sb = keep.tile([P, S // 16], U16, name="bucket_sb")
         words_all = keep.tile([P, T], U32, name="words_all", align_bytes=64)
         scales_all = keep.tile([P, T], U8, name="scales_all", align_bytes=64)
-        w1_raw = [keep.tile([P, 2, H], F32, name=f"w1_raw{u}", align_bytes=64) for u in range(2)]
+        w1_raw = [keep.tile([P, PACK, H // 2], F32, name=f"w1_raw{u}", align_bytes=64) for u in range(2)]
 
         nc.vector.memset(scales_all[:].bitcast(I32), 0)
         nc.sync.dma_start(offs_sb[:], offs)
-        w1_rows = w1.rearrange("(p u j) h -> u p j h", u=2, j=2)
+        w1_rows = w1.rearrange("(p j) (u h) -> u p j h", u=2, j=PACK)
         nc.sync.dma_start(out=w1_raw[0][:], in_=w1_rows[0])
-        for q in range(4):
-            nc.sync.dma_start(out=scales_all[32 * q : 32 * q + 4, :].bitcast(I32), in_=x_scales[0, 4 * q : 4 * q + 4, :].bitcast(I32))
+        for r in range(4):
+            nc.sync.dma_start(out=scales_all[r:P:32, :].bitcast(I32), in_=x_scales[0, r:16:4, :].bitcast(I32))
         nc.sync.dma_start(out=words_all[:].bitcast(I32), in_=x_words[0].rearrange("p n r -> p (n r)").bitcast(I32))
         nc.sync.dma_start(out=w1_raw[1][:], in_=w1_rows[1])
         nc.sync.dma_start(order_sb[:], order)
@@ -60,7 +60,7 @@ def tile_picked_lshmean_relu_p_kernel(tc, x_words, x_scales, w1, w2, offs, order
         w1_cd, w1_sc = [], []
 
         def cast_w1(t, u):
-            dst = gs[t][:].rearrange("p (b i u j) -> p u b i j", i=8, u=2, j=2)
+            dst = gs[t][:].rearrange("p (u b i j) -> p u b i j", i=8, u=2, j=PACK)
             nc.scalar.copy(out=dst[:, u], in_=w1_view[u][:, t])
 
         def quant_w1(t, g):
@@ -121,7 +121,7 @@ def tile_picked_lshmean_relu_p_kernel(tc, x_words, x_scales, w1, w2, offs, order
             d = ring.tile([P, PACK, n], F32, name="diff", tag="work")
             for t in range(PACK):
                 nc.vector.tensor_tensor(d[:, t, :], means[t][:].indirect(bucket_sb[:, c0 // 16 : (c0 + n) // 16]), y[t][:, c0 : c0 + n], ALU.subtract)
-            if c0 >= HALF:
+            if n == 128:
                 z = keep.tile([P, n * PACK], BF16, name="z_end", align_bytes=64)
             else:
                 z = ring.tile([P, n * PACK], BF16, name="z", align_bytes=64)
@@ -158,9 +158,12 @@ def tile_picked_lshmean_relu_p_kernel(tc, x_words, x_scales, w1, w2, offs, order
         for ci, n in enumerate(CHUNKS):
             last = ci == len(CHUNKS) - 1
             d, z = front(c0, n, last)
+            if not last:
+                relu(d, z, False)
             if prev is not None:
                 back(*prev)
-            relu(d, z, n == 128)
+            if last:
+                relu(d, z, True)
             prev = (c0, n, z, last)
             c0 += n
         back(*prev)

@@ -18,6 +18,7 @@ ACT = mybir.ActivationFunctionType
 P = 128
 PACK = 4
 HALF = 512
+EARLY = 1
 CHUNKS = (256, 256, 256, 128, 128)
 
 
@@ -32,36 +33,42 @@ def tile_picked_lshmean_relu_p_kernel(tc, x_words, x_scales, w1, w2, offs, order
         order_sb = keep.tile([P, S // 16], U16, name="order_sb")
         bucket_sb = keep.tile([P, S // 16], U16, name="bucket_sb")
         words_all = keep.tile([P, T], U32, name="words_all", align_bytes=64)
-        scales_all = keep.tile([P, T], U8, name="scales_all", align_bytes=64)
-        w1_raw = [keep.tile([P, PACK, H // 2], F32, name=f"w1_raw{u}", align_bytes=64) for u in range(2)]
+        scales_all = keep.tile([P, T], U8, name="scales_all", tag="scales_then_w2", align_bytes=64)
+        w1_cut = ((0, EARLY), (EARLY, PACK))
+        w1_raw = [keep.tile([P, b - a, H], F32, name=f"w1_raw{a}", align_bytes=64) for a, b in w1_cut]
 
         nc.vector.memset(scales_all[:].bitcast(I32), 0)
+        x_sc = keep.tile([P, S], U8, name="x_sc", align_bytes=64)
+        nc.vector.memset(x_sc[:].bitcast(I32), 0)
         nc.sync.dma_start(offs_sb[:], offs)
-        w1_rows = w1.rearrange("(p j) (u h) -> u p j h", u=2, j=PACK)
+        w1_all = w1.rearrange("(p j) h -> p j h", j=PACK)
+        w1_rows = [w1_all[:, a:b, :] for a, b in w1_cut]
         nc.sync.dma_start(out=w1_raw[0][:], in_=w1_rows[0])
-        for r in range(4):
-            nc.sync.dma_start(out=scales_all[r:P:32, :].bitcast(I32), in_=x_scales[0, r:16:4, :].bitcast(I32))
+        nc.sync.dma_start(out=scales_all[0:P:8, :].bitcast(I32), in_=x_scales[0].bitcast(I32))
         nc.sync.dma_start(out=words_all[:].bitcast(I32), in_=x_words[0].rearrange("p n r -> p (n r)").bitcast(I32))
         nc.sync.dma_start(out=w1_raw[1][:], in_=w1_rows[1])
         nc.sync.dma_start(order_sb[:], order)
         nc.sync.dma_start(bucket_sb[:], bucket)
-        w2_all = keep.tile([P, PACK, N], F32, name="w2_all", align_bytes=64)
+
+        picked_sc = keep.tile([P, S], U8, name="picked_sc", align_bytes=64)
+        nc.vector.tensor_copy(picked_sc[:], scales_all[:].indirect(offs_sb[:]))
+        for r in range(4):
+            nc.sync.dma_start(out=x_sc[r:P:32, :].bitcast(I32), in_=picked_sc[8 * r : P : 32, :].bitcast(I32))
+        w2_all = keep.tile([P, PACK, N], F32, name="w2_all", tag="scales_then_w2", align_bytes=64)
         w2_view = w2.rearrange("(b t i) m -> t b i m", t=PACK, i=8)
         for t in range(PACK):
             nc.sync.dma_start(out=w2_all[:, t, :], in_=w2_view[t])
 
-        x_sc = keep.tile([P, S], U8, name="x_sc", align_bytes=64)
-        nc.vector.tensor_copy(x_sc[:], scales_all[:].indirect(offs_sb[:]))
-        x_cd = [keep.tile([P, 768], U32, name="x_cd0", tag="x_cd", align_bytes=64)]
-        nc.vector.tensor_copy(x_cd[0][:], words_all[:].indirect(offs_sb[:, 0:48]))
+        x_cd = keep.tile([P, S], U32, name="x_cd", tag="x_cd", align_bytes=64)
+        nc.vector.tensor_copy(x_cd[:], words_all[:].indirect(offs_sb[:]))
 
         w1_view = [w1_raw[u][:].rearrange("p j (b t i) -> p t b i j", t=PACK, i=8) for u in range(2)]
         gs = [keep.tile([P, P * PACK], BF16, name=f"w1_g{t}", tag=f"w1_g{t}", align_bytes=64) for t in range(PACK)]
         w1_cd, w1_sc = [], []
 
         def cast_w1(t, u):
-            dst = gs[t][:].rearrange("p (u b i j) -> p u b i j", i=8, u=2, j=PACK)
-            nc.scalar.copy(out=dst[:, u], in_=w1_view[u][:, t])
+            a, b = w1_cut[u]
+            nc.scalar.copy(out=gs[t][:].rearrange("p (b i j) -> p b i j", i=8, j=PACK)[:, :, :, a:b], in_=w1_view[u][:, t])
 
         def quant_w1(t, g):
             cd = keep.tile([P, P], U32, name=f"w1_cd{t}", align_bytes=64)
@@ -73,10 +80,10 @@ def tile_picked_lshmean_relu_p_kernel(tc, x_words, x_scales, w1, w2, offs, order
         y = [keep.tile([P, S], F32, name=f"y{t}", align_bytes=64) for t in range(PACK)]
 
         def first_product(t):
-            for c0, n in ((0, 256), (256, 256), (512, 256), (768, 256)) if t == 0 else ((0, 512), (512, 256), (768, 256)):
+            for c0, n in ((0, 256), (256, 256), (512, 256), (768, 128), (896, 128)) if t == 0 else ((0, 512), (512, 512)):
                 acc = psum.tile([P, n], F32, name="acc_y", tag="acc")
                 nc.tensor.matmul_mx(out=acc[:], lhsT=w1_cd[t][:].bitcast(FP8X4), lhsT_scale=w1_sc[t][:],
-                                    rhs=x_cd[c0 // 768][:, c0 % 768 : c0 % 768 + n].bitcast(FP8X4), rhs_scale=x_sc[:, c0 : c0 + n], start=True, stop=True)
+                                    rhs=x_cd[:, c0 : c0 + n].bitcast(FP8X4), rhs_scale=x_sc[:, c0 : c0 + n], start=True, stop=True)
                 if (t, c0) == (0, HALF):
                     nc.vector.tensor_copy(out=y[t][:, c0 : c0 + n], in_=acc[:])
                 else:
@@ -85,10 +92,7 @@ def tile_picked_lshmean_relu_p_kernel(tc, x_words, x_scales, w1, w2, offs, order
         for u in range(2):
             for t in range(PACK):
                 cast_w1(t, u)
-        quant_w1(0, gs[0])
-        x_cd.append(keep.tile([P, 256], U32, name="x_cd1", tag="w1_g0", align_bytes=64))
-        nc.vector.tensor_copy(x_cd[1][:], words_all[:].indirect(offs_sb[:, 48:64]))
-        for t in range(1, PACK):
+        for t in range(PACK):
             quant_w1(t, gs[t])
         for t in range(PACK):
             first_product(t)
@@ -109,7 +113,7 @@ def tile_picked_lshmean_relu_p_kernel(tc, x_words, x_scales, w1, w2, offs, order
                                         0.5, 0.0, ALU.mult, ALU.add)
             for h in range(2):
                 vs = slice(V // 2 * h, V // 2 * (h + 1))
-                eng = nc.vector if (t, h) == (PACK - 1, 1) else nc.gpsimd
+                eng = nc.vector if t == PACK - 1 else nc.gpsimd
                 eng.tensor_tensor(out=means[t][:, vs], in0=pr[:, vs, 0], in1=pr[:, vs, 1], op=ALU.add)
         w2_cd = keep.tile([P, N], U32, name="w2_cd", align_bytes=64)
         w2_sc = keep.tile([P, N], U8, name="w2_sc", align_bytes=64)

@@ -125,7 +125,7 @@ def tile_picked_lshmean_relu_p_kernel(tc, x_words, x_scales, w1, w2, offs, order
             d = ring.tile([P, PACK, n], F32, name="diff", tag="work")
             for t in range(PACK):
                 nc.vector.tensor_tensor(d[:, t, :], means[t][:].indirect(bucket_sb[:, c0 // 16 : (c0 + n) // 16]), y[t][:, c0 : c0 + n], ALU.subtract)
-            if n == 128:
+            if c0 >= HALF:
                 z = keep.tile([P, n * PACK], BF16, name="z_end", align_bytes=64)
             else:
                 z = ring.tile([P, n * PACK], BF16, name="z", align_bytes=64)
@@ -162,12 +162,9 @@ def tile_picked_lshmean_relu_p_kernel(tc, x_words, x_scales, w1, w2, offs, order
         for ci, n in enumerate(CHUNKS):
             last = ci == len(CHUNKS) - 1
             d, z = front(c0, n, last)
-            if not last:
-                relu(d, z, False)
             if prev is not None:
                 back(*prev)
-            if last:
-                relu(d, z, True)
+            relu(d, z, n == 128)
             prev = (c0, n, z, last)
             c0 += n
         back(*prev)

@@ -102,12 +102,14 @@ def tile_picked_lshmean_relu_p_kernel(tc, x_words, x_scales, w1, w2, offs, order
 
         means = [keep.tile([P, V], F32, name=f"mean{t}", align_bytes=64) for t in range(PACK)]
 
+        work = keep.tile([P, 2 * S], F32, name="work")
         for t in range(PACK):
             if t < 2:
-                s = keep.tile([P, S], F32, name=f"lined{t}")
+                lined = keep.tile([P, S], F32, name=f"lined{t}")
+                s = lined[:]
             else:
-                s = ring.tile([P, S], F32, name="lined", tag="work")
-            pr = s[:].rearrange("p (v e) -> p v e", e=2)
+                s = work[:, S * (PACK - 1 - t) : S * (PACK - t)]
+            pr = s.rearrange("p (v e) -> p v e", e=2)
             for h in range(2):
                 nc.vector.tensor_scalar(s[:, HALF * h : HALF * (h + 1)], y[t][:].indirect(order_sb[:, 32 * h : 32 * h + 32]),
                                         0.5, 0.0, ALU.mult, ALU.add)
@@ -121,19 +123,23 @@ def tile_picked_lshmean_relu_p_kernel(tc, x_words, x_scales, w1, w2, offs, order
 
         out_view = out.rearrange("(g p) s -> p g s", p=P)
 
-        def front(c0, n, last):
-            d = ring.tile([P, PACK, n], F32, name="diff", tag="work")
-            for t in range(PACK):
-                nc.vector.tensor_tensor(d[:, t, :], means[t][:].indirect(bucket_sb[:, c0 // 16 : (c0 + n) // 16]), y[t][:, c0 : c0 + n], ALU.subtract)
-            if c0 >= HALF:
-                z = keep.tile([P, n * PACK], BF16, name="z_end", align_bytes=64)
-            else:
-                z = ring.tile([P, n * PACK], BF16, name="z", align_bytes=64)
-            return d, z
+        starts = [sum(CHUNKS[:ci]) for ci in range(len(CHUNKS))]
+        places = (S, 0, S, 0, S - CHUNKS[-1])
+        diffs = [work[:, a : a + PACK * n].rearrange("p (t n) -> p t n", t=PACK) for a, n in zip(places, CHUNKS)]
+        zs = {}
+
+        def rounded(ci):
+            zs[ci] = keep.tile([P, CHUNKS[ci] * PACK], BF16, name=f"z{ci}", tag=f"z{min(ci, 2)}", align_bytes=64)
+            return zs[ci]
+
+        def front(ci, planes):
+            c0, n = starts[ci], CHUNKS[ci]
+            for t in planes:
+                nc.vector.tensor_tensor(diffs[ci][:, t, :], means[t][:].indirect(bucket_sb[:, c0 // 16 : (c0 + n) // 16]), y[t][:, c0 : c0 + n], ALU.subtract)
 
         def relu(d, z, small):
             dst = z[:].rearrange("p (c i t) -> p c t i", i=4, t=PACK)
-            src = d[:].rearrange("p t (c i) -> p c t i", i=4)
+            src = d.rearrange("p t (c i) -> p c t i", i=4)
             if small:
                 nc.vector.tensor_scalar(dst, src, -1.0, 0.0, ALU.mult, ALU.max)
             else:
@@ -157,14 +163,16 @@ def tile_picked_lshmean_relu_p_kernel(tc, x_words, x_scales, w1, w2, offs, order
                     nc.scalar.copy(out=res[:], in_=acc[:])
                 (nc.scalar if last and u % 2 == 1 else nc.sync).dma_start(out=out_view[:, per * u : per * (u + 1), c0 : c0 + n], in_=res[:])
 
-        c0 = 0
-        prev = None
-        for ci, n in enumerate(CHUNKS):
-            last = ci == len(CHUNKS) - 1
-            d, z = front(c0, n, last)
-            if prev is not None:
-                back(*prev)
-            relu(d, z, n == 128)
-            prev = (c0, n, z, last)
-            c0 += n
-        back(*prev)
+        for ci in range(3):
+            front(ci, range(PACK))
+            if ci > 0:
+                back(starts[ci - 1], CHUNKS[ci - 1], zs[ci - 1], False)
+            relu(diffs[ci], rounded(ci), False)
+        front(3, range(PACK))
+        front(4, range(1))
+        back(starts[2], CHUNKS[2], zs[2], False)
+        relu(diffs[3], rounded(3), True)
+        front(4, range(1, PACK))
+        back(starts[3], CHUNKS[3], zs[3], False)
+        relu(diffs[4], rounded(4), True)
+        back(starts[4], CHUNKS[4], zs[4], True)

@@ -106,20 +106,19 @@ def tile_picked_lshmean_relu_p_kernel(tc, x_words, x_scales, w1, w2, offs, order
         for t in range(PACK):
             if t < 2:
                 lined = keep.tile([P, S], F32, name=f"lined{t}")
-                s = lined[:]
+                halves = [lined[:, 0:HALF], lined[:, HALF:S]]
+            elif t == 2:
+                halves = [work[:, S + HALF : 2 * S], work[:, S : S + HALF]]
             else:
-                s = work[:, S * (PACK - 1 - t) : S * (PACK - t)]
-            pr = s.rearrange("p (v e) -> p v e", e=2)
+                halves = [work[:, 0:HALF], work[:, HALF:S]]
             for h in range(2):
-                nc.vector.tensor_scalar(s[:, HALF * h : HALF * (h + 1)], y[t][:].indirect(order_sb[:, 32 * h : 32 * h + 32]),
-                                        0.5, 0.0, ALU.mult, ALU.add)
-            for h in range(2):
-                vs = slice(V // 2 * h, V // 2 * (h + 1))
-                eng = nc.vector if t == PACK - 1 else nc.gpsimd
-                eng.tensor_tensor(out=means[t][:, vs], in0=pr[:, vs, 0], in1=pr[:, vs, 1], op=ALU.add)
+                nc.vector.tensor_scalar(halves[h], y[t][:].indirect(order_sb[:, 32 * h : 32 * h + 32]), 0.5, 0.0, ALU.mult, ALU.add)
+            for h in range(2 if t < PACK - 1 else 0):
+                pr = halves[h].rearrange("p (v e) -> p v e", e=2)
+                nc.gpsimd.tensor_tensor(out=means[t][:, V // 2 * h : V // 2 * (h + 1)], in0=pr[:, :, 0], in1=pr[:, :, 1], op=ALU.add)
+        pr = work[:, 0:S].rearrange("p (v e) -> p v e", e=2)
         w2_cd = keep.tile([P, N], U32, name="w2_cd", align_bytes=64)
         w2_sc = keep.tile([P, N], U8, name="w2_sc", align_bytes=64)
-        nc.vector.quantize_mx(out=w2_cd[:].bitcast(FP8X4), scales=w2_sc[:], in_=w2_g[:])
 
         out_view = out.rearrange("(g p) s -> p g s", p=P)
 
@@ -163,8 +162,11 @@ def tile_picked_lshmean_relu_p_kernel(tc, x_words, x_scales, w1, w2, offs, order
                     nc.scalar.copy(out=res[:], in_=acc[:])
                 (nc.scalar if last and u % 2 == 1 else nc.sync).dma_start(out=out_view[:, per * u : per * (u + 1), c0 : c0 + n], in_=res[:])
 
+        front(0, range(1))
+        nc.vector.tensor_tensor(out=means[PACK - 1][:], in0=pr[:, :, 0], in1=pr[:, :, 1], op=ALU.add)
+        nc.vector.quantize_mx(out=w2_cd[:].bitcast(FP8X4), scales=w2_sc[:], in_=w2_g[:])
         for ci in range(3):
-            front(ci, range(PACK))
+            front(ci, range(1 if ci == 0 else 0, PACK))
             if ci > 0:
                 back(starts[ci - 1], CHUNKS[ci - 1], zs[ci - 1], False)
             relu(diffs[ci], rounded(ci), False)

@@ -113,10 +113,10 @@ def tile_picked_lshmean_relu_p_kernel(tc, x_words, x_scales, w1, w2, offs, order
                 halves = [work[:, 0:HALF], work[:, HALF:S]]
             for h in range(2):
                 nc.vector.tensor_scalar(halves[h], y[t][:].indirect(order_sb[:, 32 * h : 32 * h + 32]), 0.5, 0.0, ALU.mult, ALU.add)
-            for h in range(2 if t < PACK - 1 else 0):
+            for h in range(2):
                 pr = halves[h].rearrange("p (v e) -> p v e", e=2)
-                nc.gpsimd.tensor_tensor(out=means[t][:, V // 2 * h : V // 2 * (h + 1)], in0=pr[:, :, 0], in1=pr[:, :, 1], op=ALU.add)
-        pr = work[:, 0:S].rearrange("p (v e) -> p v e", e=2)
+                eng = nc.vector if t == PACK - 1 else nc.gpsimd
+                eng.tensor_tensor(out=means[t][:, V // 2 * h : V // 2 * (h + 1)], in0=pr[:, :, 0], in1=pr[:, :, 1], op=ALU.add)
         w2_cd = keep.tile([P, N], U32, name="w2_cd", align_bytes=64)
         w2_sc = keep.tile([P, N], U8, name="w2_sc", align_bytes=64)
 
@@ -162,11 +162,9 @@ def tile_picked_lshmean_relu_p_kernel(tc, x_words, x_scales, w1, w2, offs, order
                     nc.scalar.copy(out=res[:], in_=acc[:])
                 (nc.scalar if last and u % 2 == 1 else nc.sync).dma_start(out=out_view[:, per * u : per * (u + 1), c0 : c0 + n], in_=res[:])
 
-        front(0, range(1))
-        nc.vector.tensor_tensor(out=means[PACK - 1][:], in0=pr[:, :, 0], in1=pr[:, :, 1], op=ALU.add)
         nc.vector.quantize_mx(out=w2_cd[:].bitcast(FP8X4), scales=w2_sc[:], in_=w2_g[:])
         for ci in range(3):
-            front(ci, range(1 if ci == 0 else 0, PACK))
+            front(ci, range(PACK))
             if ci > 0:
                 back(starts[ci - 1], CHUNKS[ci - 1], zs[ci - 1], False)
             relu(diffs[ci], rounded(ci), False)

@@ -102,6 +102,10 @@ def tile_picked_lshmean_relu_p_kernel(tc, x_words, x_scales, w1, w2, offs, order
 
         means = [keep.tile([P, V], F32, name=f"mean{t}", align_bytes=64) for t in range(PACK)]
 
+        def pair_sum(eng, t, h, half):
+            pr = half.rearrange("p (v e) -> p v e", e=2)
+            eng.tensor_tensor(out=means[t][:, V // 2 * h : V // 2 * (h + 1)], in0=pr[:, :, 0], in1=pr[:, :, 1], op=ALU.add)
+
         work = keep.tile([P, 2 * S], F32, name="work")
         for t in range(PACK):
             if t < 2:
@@ -113,10 +117,8 @@ def tile_picked_lshmean_relu_p_kernel(tc, x_words, x_scales, w1, w2, offs, order
                 halves = [work[:, 0:HALF], work[:, HALF:S]]
             for h in range(2):
                 nc.vector.tensor_scalar(halves[h], y[t][:].indirect(order_sb[:, 32 * h : 32 * h + 32]), 0.5, 0.0, ALU.mult, ALU.add)
-            for h in range(2):
-                pr = halves[h].rearrange("p (v e) -> p v e", e=2)
-                eng = nc.vector if t == PACK - 1 else nc.gpsimd
-                eng.tensor_tensor(out=means[t][:, V // 2 * h : V // 2 * (h + 1)], in0=pr[:, :, 0], in1=pr[:, :, 1], op=ALU.add)
+            for h in range(2 if t < PACK - 1 else 1):
+                pair_sum(nc.vector if t == PACK - 1 else nc.gpsimd, t, h, halves[h])
         w2_cd = keep.tile([P, N], U32, name="w2_cd", align_bytes=64)
         w2_sc = keep.tile([P, N], U8, name="w2_sc", align_bytes=64)
 
@@ -162,9 +164,11 @@ def tile_picked_lshmean_relu_p_kernel(tc, x_words, x_scales, w1, w2, offs, order
                     nc.scalar.copy(out=res[:], in_=acc[:])
                 (nc.scalar if last and u % 2 == 1 else nc.sync).dma_start(out=out_view[:, per * u : per * (u + 1), c0 : c0 + n], in_=res[:])
 
+        front(0, range(1))
+        pair_sum(nc.vector, PACK - 1, 1, work[:, HALF:S])
         nc.vector.quantize_mx(out=w2_cd[:].bitcast(FP8X4), scales=w2_sc[:], in_=w2_g[:])
         for ci in range(3):
-            front(ci, range(PACK))
+            front(ci, range(1 if ci == 0 else 0, PACK))
             if ci > 0:
                 back(starts[ci - 1], CHUNKS[ci - 1], zs[ci - 1], False)
             relu(diffs[ci], rounded(ci), False)

@@ -42,11 +42,10 @@ def tile_picked_lshmean_relu_p_kernel(tc, x_words, x_scales, w1, w2, offs, order
         nc.vector.memset(x_sc[:].bitcast(I32), 0)
         nc.sync.dma_start(offs_sb[:], offs)
         w1_all = w1.rearrange("(p j) h -> p j h", j=PACK)
-        w1_rows = [w1_all[:, a:b, :] for a, b in w1_cut]
-        nc.sync.dma_start(out=w1_raw[0][:], in_=w1_rows[0])
+        nc.sync.dma_start(out=w1_raw[0][:], in_=w1_all[:, 0:EARLY, :])
         nc.sync.dma_start(out=scales_all[0:P:8, :].bitcast(I32), in_=x_scales[0].bitcast(I32))
         nc.sync.dma_start(out=words_all[:].bitcast(I32), in_=x_words[0].rearrange("p n r -> p (n r)").bitcast(I32))
-        nc.sync.dma_start(out=w1_raw[1][:], in_=w1_rows[1])
+        nc.sync.dma_start(out=w1_raw[1][:], in_=w1_all[:, EARLY:PACK, :])
         nc.sync.dma_start(order_sb[:], order)
         nc.sync.dma_start(bucket_sb[:], bucket)
 
@@ -59,66 +58,61 @@ def tile_picked_lshmean_relu_p_kernel(tc, x_words, x_scales, w1, w2, offs, order
         for t in range(PACK):
             nc.sync.dma_start(out=w2_all[:, t, :], in_=w2_view[t])
 
-        x_cd = keep.tile([P, S], U32, name="x_cd", tag="x_cd", align_bytes=64)
+        x_cd = keep.tile([P, S], U32, name="x_cd", align_bytes=64)
         nc.vector.tensor_copy(x_cd[:], words_all[:].indirect(offs_sb[:]))
 
-        w1_view = [w1_raw[u][:].rearrange("p j (b t i) -> p t b i j", t=PACK, i=8) for u in range(2)]
-        gs = [keep.tile([P, P * PACK], BF16, name=f"w1_g{t}", tag=f"w1_g{t}", align_bytes=64) for t in range(PACK)]
-        w1_cd, w1_sc = [], []
-
-        def cast_w1(t, u):
-            a, b = w1_cut[u]
-            nc.scalar.copy(out=gs[t][:].rearrange("p (b i j) -> p b i j", i=8, j=PACK)[:, :, :, a:b], in_=w1_view[u][:, t])
-
-        def quant_w1(t, g):
-            cd = keep.tile([P, P], U32, name=f"w1_cd{t}", align_bytes=64)
-            sc = keep.tile([P, P], U8, name=f"w1_sc{t}", align_bytes=64)
-            nc.vector.quantize_mx(out=cd[:].bitcast(FP8X4), scales=sc[:], in_=g[:])
-            w1_cd.append(cd)
-            w1_sc.append(sc)
+        w1_g = [keep.tile([P, P * PACK], BF16, name=f"w1_g{t}", align_bytes=64) for t in range(PACK)]
+        for raw, (a, b) in zip(w1_raw, w1_cut):
+            planes = raw[:].rearrange("p j (b t i) -> p t b i j", t=PACK, i=8)
+            for t in range(PACK):
+                nc.scalar.copy(out=w1_g[t][:].rearrange("p (b i j) -> p b i j", i=8, j=PACK)[:, :, :, a:b], in_=planes[:, t])
+        w1_cd = [keep.tile([P, P], U32, name=f"w1_cd{t}", align_bytes=64) for t in range(PACK)]
+        w1_sc = [keep.tile([P, P], U8, name=f"w1_sc{t}", align_bytes=64) for t in range(PACK)]
+        for t in range(PACK):
+            nc.vector.quantize_mx(out=w1_cd[t][:].bitcast(FP8X4), scales=w1_sc[t][:], in_=w1_g[t][:])
 
         y = [keep.tile([P, S], F32, name=f"y{t}", align_bytes=64) for t in range(PACK)]
+        means = [keep.tile([P, V], F32, name=f"mean{t}", align_bytes=64) for t in range(PACK)]
+        work = keep.tile([P, 2 * S], F32, name="work")
+        lined0 = keep.tile([P, S], F32, name="lined0")
+        lined1 = keep.tile([P, S], F32, name="lined1", tag="lined1_then_w2", align_bytes=64)
+        lined = [
+            [lined0[:, 0:HALF], lined0[:, HALF:S]],
+            [lined1[:, 0:HALF], lined1[:, HALF:S]],
+            [work[:, S : S + HALF], work[:, S + HALF : 2 * S]],
+            [work[:, 0:HALF], work[:, HALF:S]],
+        ]
 
         def first_product(t):
-            for c0, n in ((0, 256), (256, 256), (512, 256), (768, 128), (896, 128)) if t == 0 else ((0, 512), (512, 512)):
-                acc = psum.tile([P, n], F32, name="acc_y", tag="acc")
+            width = 256 if t == 0 else HALF
+            for k, c0 in enumerate(range(0, S, width)):
+                acc = psum.tile([P, width], F32, name="acc_y", tag="acc")
                 nc.tensor.matmul_mx(out=acc[:], lhsT=w1_cd[t][:].bitcast(FP8X4), lhsT_scale=w1_sc[t][:],
-                                    rhs=x_cd[:, c0 : c0 + n].bitcast(FP8X4), rhs_scale=x_sc[:, c0 : c0 + n], start=True, stop=True)
-                if (t, c0) == (0, HALF):
-                    nc.vector.tensor_copy(out=y[t][:, c0 : c0 + n], in_=acc[:])
+                                    rhs=x_cd[:, c0 : c0 + width].bitcast(FP8X4), rhs_scale=x_sc[:, c0 : c0 + width], start=True, stop=True)
+                if k % 2 == 0:
+                    nc.scalar.copy(out=y[t][:, c0 : c0 + width], in_=acc[:])
                 else:
-                    nc.scalar.copy(out=y[t][:, c0 : c0 + n], in_=acc[:])
+                    nc.vector.tensor_copy(out=y[t][:, c0 : c0 + width], in_=acc[:])
 
-        for u in range(2):
-            for t in range(PACK):
-                cast_w1(t, u)
-        for t in range(PACK):
-            quant_w1(t, gs[t])
-        for t in range(PACK):
-            first_product(t)
+        def line_up(t):
+            nc.scalar.activation(out=lined[t][0], in_=y[t][:].indirect(order_sb[:, 0:32]), func=ACT.Copy, scale=0.5)
+            nc.vector.tensor_scalar(lined[t][1], y[t][:].indirect(order_sb[:, 32:64]), 0.5, 0.0, ALU.mult, ALU.add)
 
-        w2_g = keep.tile([P, N * PACK], BF16, name="w2_g", tag="x_cd", align_bytes=64)
-        nc.scalar.copy(out=w2_g[:].rearrange("p (c i t) -> p c t i", i=4, t=PACK), in_=w2_all[:].rearrange("p t (c i) -> p c t i", i=4))
-
-        means = [keep.tile([P, V], F32, name=f"mean{t}", align_bytes=64) for t in range(PACK)]
-
-        def pair_sum(eng, t, h, half):
-            pr = half.rearrange("p (v e) -> p v e", e=2)
+        def pair_sum(eng, t, h):
+            pr = lined[t][h].rearrange("p (v e) -> p v e", e=2)
             eng.tensor_tensor(out=means[t][:, V // 2 * h : V // 2 * (h + 1)], in0=pr[:, :, 0], in1=pr[:, :, 1], op=ALU.add)
 
-        work = keep.tile([P, 2 * S], F32, name="work")
+        first_product(0)
         for t in range(PACK):
-            if t < 2:
-                lined = keep.tile([P, S], F32, name=f"lined{t}")
-                halves = [lined[:, 0:HALF], lined[:, HALF:S]]
-            elif t == 2:
-                halves = [work[:, S + HALF : 2 * S], work[:, S : S + HALF]]
-            else:
-                halves = [work[:, 0:HALF], work[:, HALF:S]]
-            for h in range(2):
-                nc.vector.tensor_scalar(halves[h], y[t][:].indirect(order_sb[:, 32 * h : 32 * h + 32]), 0.5, 0.0, ALU.mult, ALU.add)
-            for h in range(2 if t < PACK - 1 else 1):
-                pair_sum(nc.vector if t == PACK - 1 else nc.gpsimd, t, h, halves[h])
+            if t + 1 < PACK:
+                first_product(t + 1)
+            line_up(t)
+            if t + 1 < PACK:
+                for h in range(2):
+                    pair_sum(nc.gpsimd, t, h)
+
+        w2_g = keep.tile([P, N * PACK], BF16, name="w2_g", tag="lined1_then_w2", align_bytes=64)
+        nc.scalar.copy(out=w2_g[:].rearrange("p (c i t) -> p c t i", i=4, t=PACK), in_=w2_all[:].rearrange("p t (c i) -> p c t i", i=4))
         w2_cd = keep.tile([P, N], U32, name="w2_cd", align_bytes=64)
         w2_sc = keep.tile([P, N], U8, name="w2_sc", align_bytes=64)
 
@@ -164,13 +158,16 @@ def tile_picked_lshmean_relu_p_kernel(tc, x_words, x_scales, w1, w2, offs, order
                     nc.scalar.copy(out=res[:], in_=acc[:])
                 (nc.scalar if last and u % 2 == 1 else nc.sync).dma_start(out=out_view[:, per * u : per * (u + 1), c0 : c0 + n], in_=res[:])
 
+        pair_sum(nc.vector, PACK - 1, 0)
         front(0, range(1))
-        pair_sum(nc.vector, PACK - 1, 1, work[:, HALF:S])
+        pair_sum(nc.vector, PACK - 1, 1)
+        front(0, range(1, PACK))
+        relu(diffs[0], rounded(0), False)
+        front(1, range(1))
         nc.vector.quantize_mx(out=w2_cd[:].bitcast(FP8X4), scales=w2_sc[:], in_=w2_g[:])
-        for ci in range(3):
-            front(ci, range(1 if ci == 0 else 0, PACK))
-            if ci > 0:
-                back(starts[ci - 1], CHUNKS[ci - 1], zs[ci - 1], False)
+        for ci in range(1, 3):
+            front(ci, range(1 if ci == 1 else 0, PACK))
+            back(starts[ci - 1], CHUNKS[ci - 1], zs[ci - 1], False)
             relu(diffs[ci], rounded(ci), False)
         front(3, range(PACK))
         front(4, range(1))

@@ -73,15 +73,8 @@ def tile_picked_lshmean_relu_p_kernel(tc, x_words, x_scales, w1, w2, offs, order
 
         y = [keep.tile([P, S], F32, name=f"y{t}", align_bytes=64) for t in range(PACK)]
         means = [keep.tile([P, V], F32, name=f"mean{t}", align_bytes=64) for t in range(PACK)]
-        work = keep.tile([P, 2 * S], F32, name="work")
-        lined0 = keep.tile([P, S], F32, name="lined0")
-        lined1 = keep.tile([P, S], F32, name="lined1", tag="lined1_then_w2", align_bytes=64)
-        lined = [
-            [lined0[:, 0:HALF], lined0[:, HALF:S]],
-            [lined1[:, 0:HALF], lined1[:, HALF:S]],
-            [work[:, S : S + HALF], work[:, S + HALF : 2 * S]],
-            [work[:, 0:HALF], work[:, HALF:S]],
-        ]
+        work = keep.tile([P, 3 * S], F32, name="work")
+        lined = [keep.tile([P, S], F32, name=f"lined{t}", tag=f"lined{t}", align_bytes=64) for t in range(PACK)]
 
         def first_product(t):
             width = 256 if t == 0 else HALF
@@ -89,29 +82,32 @@ def tile_picked_lshmean_relu_p_kernel(tc, x_words, x_scales, w1, w2, offs, order
                 acc = psum.tile([P, width], F32, name="acc_y", tag="acc")
                 nc.tensor.matmul_mx(out=acc[:], lhsT=w1_cd[t][:].bitcast(FP8X4), lhsT_scale=w1_sc[t][:],
                                     rhs=x_cd[:, c0 : c0 + width].bitcast(FP8X4), rhs_scale=x_sc[:, c0 : c0 + width], start=True, stop=True)
-                if k % 2 == 0:
+                if t > 0 or k % 2 == 0:
                     nc.scalar.copy(out=y[t][:, c0 : c0 + width], in_=acc[:])
                 else:
                     nc.vector.tensor_copy(out=y[t][:, c0 : c0 + width], in_=acc[:])
 
-        def line_up(t):
-            nc.scalar.activation(out=lined[t][0], in_=y[t][:].indirect(order_sb[:, 0:32]), func=ACT.Copy, scale=0.5)
-            nc.vector.tensor_scalar(lined[t][1], y[t][:].indirect(order_sb[:, 32:64]), 0.5, 0.0, ALU.mult, ALU.add)
+        def line_up(t, h):
+            picked = y[t][:].indirect(order_sb[:, 32 * h : 32 * h + 32])
+            dst = lined[t][:, HALF * h : HALF * (h + 1)]
+            if 2 * t + h < 3:
+                nc.vector.tensor_scalar(dst, picked, 0.5, 0.0, ALU.mult, ALU.add)
+            else:
+                nc.scalar.activation(out=dst, in_=picked, func=ACT.Copy, scale=0.5)
 
-        def pair_sum(eng, t, h):
-            pr = lined[t][h].rearrange("p (v e) -> p v e", e=2)
-            eng.tensor_tensor(out=means[t][:, V // 2 * h : V // 2 * (h + 1)], in0=pr[:, :, 0], in1=pr[:, :, 1], op=ALU.add)
+        def pair_sum(eng, t, a, b):
+            pr = lined[t][:, 2 * a : 2 * b].rearrange("p (v e) -> p v e", e=2)
+            eng.tensor_tensor(out=means[t][:, a:b], in0=pr[:, :, 0], in1=pr[:, :, 1], op=ALU.add)
 
-        first_product(0)
         for t in range(PACK):
-            if t + 1 < PACK:
-                first_product(t + 1)
-            line_up(t)
-            if t + 1 < PACK:
-                for h in range(2):
-                    pair_sum(nc.gpsimd, t, h)
+            first_product(t)
+        for t in range(PACK):
+            for h in range(2):
+                line_up(t, h)
+                if t == 0:
+                    pair_sum(nc.gpsimd, t, V // 2 * h, V // 2 * (h + 1))
 
-        w2_g = keep.tile([P, N * PACK], BF16, name="w2_g", tag="lined1_then_w2", align_bytes=64)
+        w2_g = keep.tile([P, N * PACK], BF16, name="w2_g", tag="lined0", align_bytes=64)
         nc.scalar.copy(out=w2_g[:].rearrange("p (c i t) -> p c t i", i=4, t=PACK), in_=w2_all[:].rearrange("p t (c i) -> p c t i", i=4))
         w2_cd = keep.tile([P, N], U32, name="w2_cd", align_bytes=64)
         w2_sc = keep.tile([P, N], U8, name="w2_sc", align_bytes=64)
@@ -119,7 +115,7 @@ def tile_picked_lshmean_relu_p_kernel(tc, x_words, x_scales, w1, w2, offs, order
         out_view = out.rearrange("(g p) s -> p g s", p=P)
 
         starts = [sum(CHUNKS[:ci]) for ci in range(len(CHUNKS))]
-        places = (S, 0, S, 0, S - CHUNKS[-1])
+        places = (0, S, 2 * S, 0, S)
         diffs = [work[:, a : a + PACK * n].rearrange("p (t n) -> p t n", t=PACK) for a, n in zip(places, CHUNKS)]
         zs = {}
 
@@ -158,19 +154,23 @@ def tile_picked_lshmean_relu_p_kernel(tc, x_words, x_scales, w1, w2, offs, order
                     nc.scalar.copy(out=res[:], in_=acc[:])
                 (nc.scalar if last and u % 2 == 1 else nc.sync).dma_start(out=out_view[:, per * u : per * (u + 1), c0 : c0 + n], in_=res[:])
 
-        pair_sum(nc.vector, PACK - 1, 0)
-        front(0, range(1))
-        pair_sum(nc.vector, PACK - 1, 1)
-        front(0, range(1, PACK))
+        front(0, [0])
+        for t in range(1, PACK):
+            front(1, [t - 1])
+            pair_sum(nc.vector, t, 0, V)
+            front(2, [t - 1])
+            front(0, [t])
         relu(diffs[0], rounded(0), False)
-        front(1, range(1))
+        front(1, [3])
+        relu(diffs[1], rounded(1), False)
         nc.vector.quantize_mx(out=w2_cd[:].bitcast(FP8X4), scales=w2_sc[:], in_=w2_g[:])
-        for ci in range(1, 3):
-            front(ci, range(1 if ci == 1 else 0, PACK))
-            back(starts[ci - 1], CHUNKS[ci - 1], zs[ci - 1], False)
-            relu(diffs[ci], rounded(ci), False)
-        front(3, range(PACK))
-        front(4, range(1))
+        front(2, [3])
+        relu(diffs[2], rounded(2), False)
+        back(starts[0], CHUNKS[0], zs[0], False)
+        front(3, [0, 1])
+        back(starts[1], CHUNKS[1], zs[1], False)
+        front(3, [2, 3])
+        front(4, [0])
         back(starts[2], CHUNKS[2], zs[2], False)
         relu(diffs[3], rounded(3), True)
         front(4, range(1, PACK))

@@ -72,7 +72,7 @@ def tile_picked_lshmean_relu_p_kernel(tc, x_words, x_scales, w1, w2, offs, order
             nc.vector.quantize_mx(out=w1_cd[t][:].bitcast(FP8X4), scales=w1_sc[t][:], in_=w1_g[t][:])
 
         y = [keep.tile([P, S], F32, name=f"y{t}", align_bytes=64) for t in range(PACK)]
-        means = [keep.tile([P, V], F32, name=f"mean{t}", align_bytes=64) for t in range(PACK)]
+        means = {t: keep.tile([P, V], F32, name=f"mean{t}", align_bytes=64) for t in (0, 2, 3)}
         work = keep.tile([P, 3 * S], F32, name="work")
         lined = [keep.tile([P, S], F32, name=f"lined{t}", tag=f"lined{t}", align_bytes=64) for t in range(PACK)]
 
@@ -82,7 +82,7 @@ def tile_picked_lshmean_relu_p_kernel(tc, x_words, x_scales, w1, w2, offs, order
                 acc = psum.tile([P, width], F32, name="acc_y", tag="acc")
                 nc.tensor.matmul_mx(out=acc[:], lhsT=w1_cd[t][:].bitcast(FP8X4), lhsT_scale=w1_sc[t][:],
                                     rhs=x_cd[:, c0 : c0 + width].bitcast(FP8X4), rhs_scale=x_sc[:, c0 : c0 + width], start=True, stop=True)
-                if t > 0 or k % 2 == 0:
+                if (t, k) != (0, 1):
                     nc.scalar.copy(out=y[t][:, c0 : c0 + width], in_=acc[:])
                 else:
                     nc.vector.tensor_copy(out=y[t][:, c0 : c0 + width], in_=acc[:])
@@ -90,7 +90,7 @@ def tile_picked_lshmean_relu_p_kernel(tc, x_words, x_scales, w1, w2, offs, order
         def line_up(t, h):
             picked = y[t][:].indirect(order_sb[:, 32 * h : 32 * h + 32])
             dst = lined[t][:, HALF * h : HALF * (h + 1)]
-            if 2 * t + h < 3:
+            if (t, h) in ((0, 0), (1, 0), (1, 1)):
                 nc.vector.tensor_scalar(dst, picked, 0.5, 0.0, ALU.mult, ALU.add)
             else:
                 nc.scalar.activation(out=dst, in_=picked, func=ACT.Copy, scale=0.5)
@@ -99,15 +99,20 @@ def tile_picked_lshmean_relu_p_kernel(tc, x_words, x_scales, w1, w2, offs, order
             pr = lined[t][:, 2 * a : 2 * b].rearrange("p (v e) -> p v e", e=2)
             eng.tensor_tensor(out=means[t][:, a:b], in0=pr[:, :, 0], in1=pr[:, :, 1], op=ALU.add)
 
-        for t in range(PACK):
+        for t in range(2):
             first_product(t)
-        for t in range(PACK):
+        for h in range(2):
+            line_up(0, h)
+        for h in range(2):
+            pair_sum(nc.gpsimd, 0, V // 2 * h, V // 2 * (h + 1))
+        means[1] = keep.tile([P, V], F32, name="mean1", tag="lined0", align_bytes=64)
+        for t in range(2, PACK):
+            first_product(t)
+        for t in range(1, PACK):
             for h in range(2):
                 line_up(t, h)
-                if t == 0:
-                    pair_sum(nc.gpsimd, t, V // 2 * h, V // 2 * (h + 1))
 
-        w2_g = keep.tile([P, N * PACK], BF16, name="w2_g", tag="lined0", align_bytes=64)
+        w2_g = keep.tile([P, N * PACK], BF16, name="w2_g", tag="lined1", align_bytes=64)
         nc.scalar.copy(out=w2_g[:].rearrange("p (c i t) -> p c t i", i=4, t=PACK), in_=w2_all[:].rearrange("p t (c i) -> p c t i", i=4))
         w2_cd = keep.tile([P, N], U32, name="w2_cd", align_bytes=64)
         w2_sc = keep.tile([P, N], U8, name="w2_sc", align_bytes=64)
@@ -155,11 +160,17 @@ def tile_picked_lshmean_relu_p_kernel(tc, x_words, x_scales, w1, w2, offs, order
                 (nc.scalar if last and u % 2 == 1 else nc.sync).dma_start(out=out_view[:, per * u : per * (u + 1), c0 : c0 + n], in_=res[:])
 
         front(0, [0])
-        for t in range(1, PACK):
-            front(1, [t - 1])
+        pair_sum(nc.vector, 1, 0, V)
+        front(1, [0])
+        front(0, [1])
+        front(1, [1])
+        front(2, [0])
+        for t in range(2, PACK):
             pair_sum(nc.vector, t, 0, V)
             front(2, [t - 1])
             front(0, [t])
+            if t < PACK - 1:
+                front(1, [t])
         relu(diffs[0], rounded(0), False)
         front(1, [3])
         relu(diffs[1], rounded(1), False)

@@ -141,23 +141,33 @@ def tile_picked_lshmean_relu_p_kernel(tc, x_words, x_scales, w1, w2, offs, order
             else:
                 nc.scalar.activation(out=dst, in_=src, func=ACT.Relu, scale=-1.0)
 
-        def back(c0, n, z, last):
+        def product(n, z, per):
             z_cd = ring.tile([P, n], U32, name="z_cd", align_bytes=64)
             z_sc = ring.tile([P, n], U8, name="z_sc", align_bytes=64)
             nc.vector.quantize_mx(out=z_cd[:].bitcast(FP8X4), scales=z_sc[:], in_=z[:])
-            per = 1 if last else 2
+            banks = []
             for u in range(PACK // per):
                 acc = psum.tile([P, per, n], F32, name="acc_o", tag="acc")
                 for k in range(per):
                     g = per * u + k
                     nc.tensor.matmul_mx(out=acc[:, k, :], lhsT=w2_cd[:, P * g : P * (g + 1)].bitcast(FP8X4), lhsT_scale=w2_sc[:, P * g : P * (g + 1)],
                                         rhs=z_cd[:].bitcast(FP8X4), rhs_scale=z_sc[:], start=True, stop=True)
-                res = keep.tile([P, per, n], F32, name=f"res{c0}_{u}")
-                if last and u % 2 == 0:
-                    nc.vector.tensor_copy(out=res[:], in_=acc[:])
-                else:
-                    nc.scalar.copy(out=res[:], in_=acc[:])
-                (nc.scalar if last and u % 2 == 1 else nc.sync).dma_start(out=out_view[:, per * u : per * (u + 1), c0 : c0 + n], in_=res[:])
+                banks.append(acc)
+            return banks
+
+        def leave(c0, n, banks, u, on_vector, queue, tag=None):
+            per = PACK // len(banks)
+            res = keep.tile([P, per, n], F32, name=f"res{c0}_{u}", tag=tag or f"res{c0}_{u}", align_bytes=64)
+            if on_vector:
+                nc.vector.tensor_copy(out=res[:], in_=banks[u][:])
+            else:
+                nc.scalar.copy(out=res[:], in_=banks[u][:])
+            queue.dma_start(out=out_view[:, per * u : per * (u + 1), c0 : c0 + n], in_=res[:])
+
+        def back(c0, n, z):
+            banks = product(n, z, 2)
+            for u in range(2):
+                leave(c0, n, banks, u, False, nc.sync)
 
         front(0, [0])
         pair_sum(nc.vector, 1, 0, V)
@@ -165,26 +175,32 @@ def tile_picked_lshmean_relu_p_kernel(tc, x_words, x_scales, w1, w2, offs, order
         front(0, [1])
         front(1, [1])
         front(2, [0])
-        for t in range(2, PACK):
-            pair_sum(nc.vector, t, 0, V)
-            front(2, [t - 1])
-            front(0, [t])
-            if t < PACK - 1:
-                front(1, [t])
+        pair_sum(nc.vector, 2, 0, V)
+        front(2, [1])
+        front(0, [2])
+        for h in range(2):
+            pair_sum(nc.vector, 3, V // 2 * h, V // 2 * (h + 1))
+        front(1, [2])
+        front(0, [3])
         relu(diffs[0], rounded(0), False)
         front(1, [3])
         relu(diffs[1], rounded(1), False)
+        front(2, [2])
         nc.vector.quantize_mx(out=w2_cd[:].bitcast(FP8X4), scales=w2_sc[:], in_=w2_g[:])
         front(2, [3])
         relu(diffs[2], rounded(2), False)
-        back(starts[0], CHUNKS[0], zs[0], False)
+        back(starts[0], CHUNKS[0], zs[0])
         front(3, [0, 1])
-        back(starts[1], CHUNKS[1], zs[1], False)
+        back(starts[1], CHUNKS[1], zs[1])
         front(3, [2, 3])
         front(4, [0])
-        back(starts[2], CHUNKS[2], zs[2], False)
+        back(starts[2], CHUNKS[2], zs[2])
         relu(diffs[3], rounded(3), True)
         front(4, range(1, PACK))
-        back(starts[3], CHUNKS[3], zs[3], False)
+        fourth = product(CHUNKS[3], zs[3], 2)
+        leave(starts[3], CHUNKS[3], fourth, 0, False, nc.sync)
         relu(diffs[4], rounded(4), True)
-        back(starts[4], CHUNKS[4], zs[4], True)
+        fifth = product(CHUNKS[4], zs[4], 1)
+        leave(starts[3], CHUNKS[3], fourth, 1, True, nc.sync, "z2")
+        for u in range(PACK):
+            leave(starts[4], CHUNKS[4], fifth, u, u % 2 == 0, nc.scalar if u % 2 == 1 else nc.sync)

@@ -61,15 +61,19 @@ def tile_picked_lshmean_relu_p_kernel(tc, x_words, x_scales, w1, w2, offs, order
         x_cd = keep.tile([P, S], U32, name="x_cd", align_bytes=64)
         nc.vector.tensor_copy(x_cd[:], words_all[:].indirect(offs_sb[:]))
 
-        w1_g = [keep.tile([P, P * PACK], BF16, name=f"w1_g{t}", align_bytes=64) for t in range(PACK)]
+        w1_all_g = keep.tile([P, PACK, P * PACK], BF16, name="w1_g", align_bytes=64)
+        w1_g = [w1_all_g[:, t, :] for t in range(PACK)]
         for raw, (a, b) in zip(w1_raw, w1_cut):
             planes = raw[:].rearrange("p j (b t i) -> p t b i j", t=PACK, i=8)
             for t in range(PACK):
-                nc.scalar.copy(out=w1_g[t][:].rearrange("p (b i j) -> p b i j", i=8, j=PACK)[:, :, :, a:b], in_=planes[:, t])
-        w1_cd = [keep.tile([P, P], U32, name=f"w1_cd{t}", align_bytes=64) for t in range(PACK)]
-        w1_sc = [keep.tile([P, P], U8, name=f"w1_sc{t}", align_bytes=64) for t in range(PACK)]
-        for t in range(PACK):
-            nc.vector.quantize_mx(out=w1_cd[t][:].bitcast(FP8X4), scales=w1_sc[t][:], in_=w1_g[t][:])
+                nc.scalar.copy(out=w1_g[t].rearrange("p (b i j) -> p b i j", i=8, j=PACK)[:, :, :, a:b], in_=planes[:, t])
+        w1_codes = keep.tile([P, H], U32, name="w1_codes", align_bytes=64)
+        w1_bytes = keep.tile([P, H], U8, name="w1_bytes", align_bytes=64)
+        w1_cd = [w1_codes[:, P * t : P * (t + 1)] for t in range(PACK)]
+        w1_sc = [w1_bytes[:, P * t : P * (t + 1)] for t in range(PACK)]
+        for a, b in ((0, 1), (1, 3), (3, 4)):
+            nc.vector.quantize_mx(out=w1_codes[:, P * a : P * b].bitcast(FP8X4), scales=w1_bytes[:, P * a : P * b],
+                                  in_=w1_all_g[:, a:b, :].rearrange("p t c -> p (t c)"))
 
         y = [keep.tile([P, S], F32, name=f"y{t}", align_bytes=64) for t in range(PACK)]
         means = {t: keep.tile([P, V], F32, name=f"mean{t}", align_bytes=64) for t in (0, 2, 3)}
@@ -80,7 +84,7 @@ def tile_picked_lshmean_relu_p_kernel(tc, x_words, x_scales, w1, w2, offs, order
             width = 256 if t == 0 else HALF
             for k, c0 in enumerate(range(0, S, width)):
                 acc = psum.tile([P, width], F32, name="acc_y", tag="acc")
-                nc.tensor.matmul_mx(out=acc[:], lhsT=w1_cd[t][:].bitcast(FP8X4), lhsT_scale=w1_sc[t][:],
+                nc.tensor.matmul_mx(out=acc[:], lhsT=w1_cd[t].bitcast(FP8X4), lhsT_scale=w1_sc[t],
                                     rhs=x_cd[:, c0 : c0 + width].bitcast(FP8X4), rhs_scale=x_sc[:, c0 : c0 + width], start=True, stop=True)
                 if (t, k) != (0, 1):
                     nc.scalar.copy(out=y[t][:, c0 : c0 + width], in_=acc[:])
@@ -122,11 +126,9 @@ def tile_picked_lshmean_relu_p_kernel(tc, x_words, x_scales, w1, w2, offs, order
         starts = [sum(CHUNKS[:ci]) for ci in range(len(CHUNKS))]
         places = (0, S, 2 * S, 0, S)
         diffs = [work[:, a : a + PACK * n].rearrange("p (t n) -> p t n", t=PACK) for a, n in zip(places, CHUNKS)]
-        zs = {}
-
-        def rounded(ci):
-            zs[ci] = keep.tile([P, CHUNKS[ci] * PACK], BF16, name=f"z{ci}", tag=f"z{min(ci, 2)}", align_bytes=64)
-            return zs[ci]
+        z_a = keep.tile([P, 3 * HALF], BF16, name="z_a", align_bytes=64)
+        z_b = keep.tile([P, 2 * HALF], BF16, name="z_b", align_bytes=64)
+        zs = [z_a[:, HALF:], z_b[:], z_a[:, : 2 * HALF], z_a[:, :HALF], z_a[:, :HALF]]
 
         def front(ci, planes):
             c0, n = starts[ci], CHUNKS[ci]
@@ -134,7 +136,7 @@ def tile_picked_lshmean_relu_p_kernel(tc, x_words, x_scales, w1, w2, offs, order
                 nc.vector.tensor_tensor(diffs[ci][:, t, :], means[t][:].indirect(bucket_sb[:, c0 // 16 : (c0 + n) // 16]), y[t][:, c0 : c0 + n], ALU.subtract)
 
         def relu(d, z, small):
-            dst = z[:].rearrange("p (c i t) -> p c t i", i=4, t=PACK)
+            dst = z.rearrange("p (c i t) -> p c t i", i=4, t=PACK)
             src = d.rearrange("p t (c i) -> p c t i", i=4)
             if small:
                 nc.vector.tensor_scalar(dst, src, -1.0, 0.0, ALU.mult, ALU.max)
@@ -144,7 +146,7 @@ def tile_picked_lshmean_relu_p_kernel(tc, x_words, x_scales, w1, w2, offs, order
         def product(n, z, per):
             z_cd = ring.tile([P, n], U32, name="z_cd", align_bytes=64)
             z_sc = ring.tile([P, n], U8, name="z_sc", align_bytes=64)
-            nc.vector.quantize_mx(out=z_cd[:].bitcast(FP8X4), scales=z_sc[:], in_=z[:])
+            nc.vector.quantize_mx(out=z_cd[:].bitcast(FP8X4), scales=z_sc[:], in_=z)
             banks = []
             for u in range(PACK // per):
                 acc = psum.tile([P, per, n], F32, name="acc_o", tag="acc")
@@ -155,14 +157,15 @@ def tile_picked_lshmean_relu_p_kernel(tc, x_words, x_scales, w1, w2, offs, order
                 banks.append(acc)
             return banks
 
-        def leave(c0, n, banks, u, on_vector, queue, tag=None):
+        def leave(c0, n, banks, u, on_vector, queue, res=None):
             per = PACK // len(banks)
-            res = keep.tile([P, per, n], F32, name=f"res{c0}_{u}", tag=tag or f"res{c0}_{u}", align_bytes=64)
+            if res is None:
+                res = keep.tile([P, per, n], F32, name=f"res{c0}_{u}", align_bytes=64)[:]
             if on_vector:
-                nc.vector.tensor_copy(out=res[:], in_=banks[u][:])
+                nc.vector.tensor_copy(out=res, in_=banks[u][:])
             else:
-                nc.scalar.copy(out=res[:], in_=banks[u][:])
-            queue.dma_start(out=out_view[:, per * u : per * (u + 1), c0 : c0 + n], in_=res[:])
+                nc.scalar.copy(out=res, in_=banks[u][:])
+            queue.dma_start(out=out_view[:, per * u : per * (u + 1), c0 : c0 + n], in_=res)
 
         def back(c0, n, z):
             banks = product(n, z, 2)
@@ -182,25 +185,28 @@ def tile_picked_lshmean_relu_p_kernel(tc, x_words, x_scales, w1, w2, offs, order
             pair_sum(nc.vector, 3, V // 2 * h, V // 2 * (h + 1))
         front(1, [2])
         front(0, [3])
-        relu(diffs[0], rounded(0), False)
+        relu(diffs[0], zs[0], False)
         front(1, [3])
-        relu(diffs[1], rounded(1), False)
+        relu(diffs[1], zs[1], False)
         front(2, [2])
         nc.vector.quantize_mx(out=w2_cd[:].bitcast(FP8X4), scales=w2_sc[:], in_=w2_g[:])
         front(2, [3])
-        relu(diffs[2], rounded(2), False)
+        half = CHUNKS[2] // 2
+        relu(diffs[2][:, :, :half], zs[2][:, :HALF], False)
         back(starts[0], CHUNKS[0], zs[0])
-        front(3, [0, 1])
+        front(3, [0])
+        relu(diffs[2][:, :, half:], zs[2][:, HALF:], True)
+        front(3, [1])
         back(starts[1], CHUNKS[1], zs[1])
         front(3, [2, 3])
         front(4, [0])
         back(starts[2], CHUNKS[2], zs[2])
-        relu(diffs[3], rounded(3), True)
+        relu(diffs[3], zs[3], True)
         front(4, range(1, PACK))
         fourth = product(CHUNKS[3], zs[3], 2)
         leave(starts[3], CHUNKS[3], fourth, 0, False, nc.sync)
-        relu(diffs[4], rounded(4), True)
+        relu(diffs[4], zs[4], True)
         fifth = product(CHUNKS[4], zs[4], 1)
-        leave(starts[3], CHUNKS[3], fourth, 1, True, nc.sync, "z2")
+        leave(starts[3], CHUNKS[3], fourth, 1, True, nc.sync, zs[4].bitcast(F32).rearrange("p (g n) -> p g n", g=2))
         for u in range(PACK):
             leave(starts[4], CHUNKS[4], fifth, u, u % 2 == 0, nc.scalar if u % 2 == 1 else nc.sync)

@@ -124,16 +124,16 @@ def tile_picked_lshmean_relu_p_kernel(tc, x_words, x_scales, w1, w2, offs, order
         out_view = out.rearrange("(g p) s -> p g s", p=P)
 
         starts = [sum(CHUNKS[:ci]) for ci in range(len(CHUNKS))]
-        places = (0, S, 2 * S, 0, S)
-        diffs = [work[:, a : a + PACK * n].rearrange("p (t n) -> p t n", t=PACK) for a, n in zip(places, CHUNKS)]
+        diffs = [work[:, S * ci : S * (ci + 1)].rearrange("p (t n) -> p t n", t=PACK) for ci in range(3)]
+        diffs += [diffs[0][:, :, : CHUNKS[3]], diffs[0][:, :, CHUNKS[3] :]]
         z_a = keep.tile([P, 3 * HALF], BF16, name="z_a", align_bytes=64)
         z_b = keep.tile([P, 2 * HALF], BF16, name="z_b", align_bytes=64)
-        zs = [z_a[:, HALF:], z_b[:], z_a[:, : 2 * HALF], z_a[:, :HALF], z_a[:, :HALF]]
+        zs = [z_a[:, HALF:], z_b[:], z_a[:, : 2 * HALF], z_a[:, :HALF], z_a[:, HALF : 2 * HALF]]
 
-        def front(ci, planes):
-            c0, n = starts[ci], CHUNKS[ci]
+        def front(ci, planes, both=False):
+            c0, n = starts[ci], CHUNKS[0] if both else CHUNKS[ci]
             for t in planes:
-                nc.vector.tensor_tensor(diffs[ci][:, t, :], means[t][:].indirect(bucket_sb[:, c0 // 16 : (c0 + n) // 16]), y[t][:, c0 : c0 + n], ALU.subtract)
+                nc.vector.tensor_tensor(diffs[0 if both else ci][:, t, :], means[t][:].indirect(bucket_sb[:, c0 // 16 : (c0 + n) // 16]), y[t][:, c0 : c0 + n], ALU.subtract)
 
         def relu(d, z, small):
             dst = z.rearrange("p (c i t) -> p c t i", i=4, t=PACK)
@@ -194,19 +194,19 @@ def tile_picked_lshmean_relu_p_kernel(tc, x_words, x_scales, w1, w2, offs, order
         half = CHUNKS[2] // 2
         relu(diffs[2][:, :, :half], zs[2][:, :HALF], False)
         back(starts[0], CHUNKS[0], zs[0])
-        front(3, [0])
+        front(3, [0], True)
         relu(diffs[2][:, :, half:], zs[2][:, HALF:], True)
-        front(3, [1])
         back(starts[1], CHUNKS[1], zs[1])
-        front(3, [2, 3])
-        front(4, [0])
+        front(3, [1], True)
         back(starts[2], CHUNKS[2], zs[2])
-        relu(diffs[3], zs[3], True)
-        front(4, range(1, PACK))
+        front(3, [2], True)
+        for ci in (3, 4):
+            front(ci, [3])
+        for ci in (3, 4):
+            relu(diffs[ci], zs[ci], True)
         fourth = product(CHUNKS[3], zs[3], 2)
-        leave(starts[3], CHUNKS[3], fourth, 0, False, nc.sync)
-        relu(diffs[4], zs[4], True)
         fifth = product(CHUNKS[4], zs[4], 1)
-        leave(starts[3], CHUNKS[3], fourth, 1, True, nc.sync, zs[4].bitcast(F32).rearrange("p (g n) -> p g n", g=2))
+        for u in range(2):
+            leave(starts[3], CHUNKS[3], fourth, u, u == 1, nc.sync)
         for u in range(PACK):
-            leave(starts[4], CHUNKS[4], fifth, u, u % 2 == 0, nc.scalar if u % 2 == 1 else nc.sync)
+            leave(starts[4], CHUNKS[4], fifth, u, u % 2 == 1, nc.scalar if u % 2 == 0 else nc.sync)

@@ -18,6 +18,8 @@ ACT = mybir.ActivationFunctionType
 P = 128
 PACK = 4
 HALF = 512
+ROW_START = 256
+SHARE = 96
 EARLY = 1
 CHUNKS = (256, 256, 256, 128, 128)
 
@@ -32,10 +34,10 @@ def tile_picked_lshmean_relu_p_kernel(tc, x_words, x_scales, w1, w2, offs, order
         offs_sb = keep.tile([P, S // 16], U16, name="offs_sb")
         order_sb = keep.tile([P, S // 16], U16, name="order_sb")
         bucket_sb = keep.tile([P, S // 16], U16, name="bucket_sb")
-        words_all = keep.tile([P, T], U32, name="words_all", align_bytes=64)
-        scales_all = keep.tile([P, T], U8, name="scales_all", tag="scales_then_w2", align_bytes=64)
+        words_all = keep.tile([P, T], U32, name="words_all", align_bytes=ROW_START)
+        scales_all = keep.tile([P, T], U8, name="scales_all", tag="scales_then_w2", align_bytes=ROW_START)
         w1_cut = ((0, EARLY), (EARLY, PACK))
-        w1_raw = [keep.tile([P, b - a, H], F32, name=f"w1_raw{a}", align_bytes=64) for a, b in w1_cut]
+        w1_raw = [keep.tile([P, b - a, H], F32, name=f"w1_raw{a}", align_bytes=ROW_START) for a, b in w1_cut]
 
         nc.vector.memset(scales_all[:].bitcast(I32), 0)
         x_sc = keep.tile([P, S], U8, name="x_sc", align_bytes=64)
@@ -53,7 +55,7 @@ def tile_picked_lshmean_relu_p_kernel(tc, x_words, x_scales, w1, w2, offs, order
         nc.vector.tensor_copy(picked_sc[:], scales_all[:].indirect(offs_sb[:]))
         for r in range(4):
             nc.sync.dma_start(out=x_sc[r:P:32, :].bitcast(I32), in_=picked_sc[8 * r : P : 32, :].bitcast(I32))
-        w2_all = keep.tile([P, PACK, N], F32, name="w2_all", tag="scales_then_w2", align_bytes=64)
+        w2_all = keep.tile([P, PACK, N], F32, name="w2_all", tag="scales_then_w2", align_bytes=ROW_START)
         w2_view = w2.rearrange("(b t i) m -> t b i m", t=PACK, i=8)
         for t in range(PACK):
             nc.sync.dma_start(out=w2_all[:, t, :], in_=w2_view[t])
@@ -124,16 +126,19 @@ def tile_picked_lshmean_relu_p_kernel(tc, x_words, x_scales, w1, w2, offs, order
         out_view = out.rearrange("(g p) s -> p g s", p=P)
 
         starts = [sum(CHUNKS[:ci]) for ci in range(len(CHUNKS))]
-        diffs = [work[:, S * ci : S * (ci + 1)].rearrange("p (t n) -> p t n", t=PACK) for ci in range(3)]
-        diffs += [diffs[0][:, :, : CHUNKS[3]], diffs[0][:, :, CHUNKS[3] :]]
-        z_a = keep.tile([P, 3 * HALF], BF16, name="z_a", align_bytes=64)
+        places = (0, 2 * S, S, S - CHUNKS[0])
+        diffs = [work[:, a : a + S].rearrange("p (t n) -> p t n", t=PACK) for a in places]
+        joint = diffs.pop()
+        diffs += [joint[:, :, : CHUNKS[3]], joint[:, :, CHUNKS[3] :]]
+        cut = CHUNKS[2] - SHARE
+        z_a = keep.tile([P, 2 * HALF + cut * PACK], BF16, name="z_a", align_bytes=64)
         z_b = keep.tile([P, 2 * HALF], BF16, name="z_b", align_bytes=64)
-        zs = [z_a[:, HALF:], z_b[:], z_a[:, : 2 * HALF], z_a[:, :HALF], z_a[:, HALF : 2 * HALF]]
+        zs = [z_a[:, cut * PACK :], z_b[:], z_a[:, : 2 * HALF], z_a[:, :HALF], z_a[:, HALF : 2 * HALF]]
 
         def front(ci, planes, both=False):
             c0, n = starts[ci], CHUNKS[0] if both else CHUNKS[ci]
             for t in planes:
-                nc.vector.tensor_tensor(diffs[0 if both else ci][:, t, :], means[t][:].indirect(bucket_sb[:, c0 // 16 : (c0 + n) // 16]), y[t][:, c0 : c0 + n], ALU.subtract)
+                nc.vector.tensor_tensor((joint if both else diffs[ci])[:, t, :], means[t][:].indirect(bucket_sb[:, c0 // 16 : (c0 + n) // 16]), y[t][:, c0 : c0 + n], ALU.subtract)
 
         def relu(d, z, small):
             dst = z.rearrange("p (c i t) -> p c t i", i=4, t=PACK)
@@ -157,10 +162,9 @@ def tile_picked_lshmean_relu_p_kernel(tc, x_words, x_scales, w1, w2, offs, order
                 banks.append(acc)
             return banks
 
-        def leave(c0, n, banks, u, on_vector, queue, res=None):
+        def leave(c0, n, banks, u, on_vector, queue):
             per = PACK // len(banks)
-            if res is None:
-                res = keep.tile([P, per, n], F32, name=f"res{c0}_{u}", align_bytes=64)[:]
+            res = keep.tile([P, per, n], F32, name=f"res{c0}_{u}", align_bytes=ROW_START)[:]
             if on_vector:
                 nc.vector.tensor_copy(out=res, in_=banks[u][:])
             else:
@@ -191,11 +195,10 @@ def tile_picked_lshmean_relu_p_kernel(tc, x_words, x_scales, w1, w2, offs, order
         front(2, [2])
         nc.vector.quantize_mx(out=w2_cd[:].bitcast(FP8X4), scales=w2_sc[:], in_=w2_g[:])
         front(2, [3])
-        half = CHUNKS[2] // 2
-        relu(diffs[2][:, :, :half], zs[2][:, :HALF], False)
+        relu(diffs[2][:, :, :cut], zs[2][:, : cut * PACK], False)
         back(starts[0], CHUNKS[0], zs[0])
         front(3, [0], True)
-        relu(diffs[2][:, :, half:], zs[2][:, HALF:], True)
+        relu(diffs[2][:, :, cut:], zs[2][:, cut * PACK :], True)
         back(starts[1], CHUNKS[1], zs[1])
         front(3, [1], True)
         back(starts[2], CHUNKS[2], zs[2])

from contextlib import ExitStack

import concourse.mybir as mybir

K, T, S, V, N, H = 512, 2048, 1024, 512, 512, 512
FLOPS = 2 * K * H * S + 2 * H * N * S

F32 = mybir.dt.float32
BF16 = mybir.dt.bfloat16
I32 = mybir.dt.int32
U32 = mybir.dt.uint32
U16 = mybir.dt.uint16
U8 = mybir.dt.uint8
FP8X4 = mybir.dt.float8_e4m3fn_x4
ALU = mybir.AluOpType
ACT = mybir.ActivationFunctionType

P = 128
PACK = 4
HALF = 512
ROW_START = 256
SHARE = 96
EARLY = 1
CHUNKS = (256, 256, 256, 128, 128)


def tile_picked_lshmean_relu_p_kernel(tc, x_words, x_scales, w1, w2, offs, order, bucket, out):
    nc = tc.nc
    with ExitStack() as ctx:
        keep = ctx.enter_context(tc.tile_pool(name="keep", bufs=1))
        ring = ctx.enter_context(tc.tile_pool(name="ring", bufs=2))
        psum = ctx.enter_context(tc.psum_pool(name="psum", bufs=8))

        offs_sb = keep.tile([P, S // 16], U16, name="offs_sb")
        order_sb = keep.tile([P, S // 16], U16, name="order_sb")
        bucket_sb = keep.tile([P, S // 16], U16, name="bucket_sb")
        words_all = keep.tile([P, T], U32, name="words_all", align_bytes=ROW_START)
        scales_all = keep.tile([P, T], U8, name="scales_all", tag="scales_then_w2", align_bytes=ROW_START)
        w1_cut = ((0, EARLY), (EARLY, PACK))
        w1_raw = [keep.tile([P, b - a, H], F32, name=f"w1_raw{a}", align_bytes=ROW_START) for a, b in w1_cut]

        nc.vector.memset(scales_all[:].bitcast(I32), 0)
        x_sc = keep.tile([P, S], U8, name="x_sc", align_bytes=64)
        nc.vector.memset(x_sc[:].bitcast(I32), 0)
        nc.sync.dma_start(offs_sb[:], offs)
        w1_all = w1.rearrange("(p j) h -> p j h", j=PACK)
        nc.sync.dma_start(out=w1_raw[0][:], in_=w1_all[:, 0:EARLY, :])
        nc.sync.dma_start(out=scales_all[0:P:8, :].bitcast(I32), in_=x_scales[0].bitcast(I32))
        nc.sync.dma_start(out=words_all[:].bitcast(I32), in_=x_words[0].rearrange("p n r -> p (n r)").bitcast(I32))
        nc.sync.dma_start(out=w1_raw[1][:], in_=w1_all[:, EARLY:PACK, :])
        nc.sync.dma_start(order_sb[:], order)
        nc.sync.dma_start(bucket_sb[:], bucket)

        picked_sc = keep.tile([P, S], U8, name="picked_sc", align_bytes=64)
        nc.vector.tensor_copy(picked_sc[:], scales_all[:].indirect(offs_sb[:]))
        for r in range(4):
            nc.sync.dma_start(out=x_sc[r:P:32, :].bitcast(I32), in_=picked_sc[8 * r : P : 32, :].bitcast(I32))
        w2_all = keep.tile([P, PACK, N], F32, name="w2_all", tag="scales_then_w2", align_bytes=ROW_START)
        w2_view = w2.rearrange("(b t i) m -> t b i m", t=PACK, i=8)
        for t in range(PACK):
            nc.sync.dma_start(out=w2_all[:, t, :], in_=w2_view[t])

        x_cd = keep.tile([P, S], U32, name="x_cd", align_bytes=64)
        nc.vector.tensor_copy(x_cd[:], words_all[:].indirect(offs_sb[:]))

        w1_all_g = keep.tile([P, PACK, P * PACK], BF16, name="w1_g", align_bytes=64)
        w1_g = [w1_all_g[:, t, :] for t in range(PACK)]
        for raw, (a, b) in zip(w1_raw, w1_cut):
            planes = raw[:].rearrange("p j (b t i) -> p t b i j", t=PACK, i=8)
            for t in range(PACK):
                nc.scalar.copy(out=w1_g[t].rearrange("p (b i j) -> p b i j", i=8, j=PACK)[:, :, :, a:b], in_=planes[:, t])
        w1_codes = keep.tile([P, H], U32, name="w1_codes", align_bytes=64)
        w1_bytes = keep.tile([P, H], U8, name="w1_bytes", align_bytes=64)
        w1_cd = [w1_codes[:, P * t : P * (t + 1)] for t in range(PACK)]
        w1_sc = [w1_bytes[:, P * t : P * (t + 1)] for t in range(PACK)]
        for a, b in ((0, 1), (1, 3), (3, 4)):
            nc.vector.quantize_mx(out=w1_codes[:, P * a : P * b].bitcast(FP8X4), scales=w1_bytes[:, P * a : P * b],
                                  in_=w1_all_g[:, a:b, :].rearrange("p t c -> p (t c)"))

        y = [keep.tile([P, S], F32, name=f"y{t}", align_bytes=64) for t in range(PACK)]
        means = {t: keep.tile([P, V], F32, name=f"mean{t}", align_bytes=64) for t in (0, 2, 3)}
        work = keep.tile([P, 3 * S], F32, name="work")
        lined = [keep.tile([P, S], F32, name=f"lined{t}", tag=f"lined{t}", align_bytes=64) for t in range(PACK)]

        def first_product(t):
            width = 256 if t == 0 else HALF
            for k, c0 in enumerate(range(0, S, width)):
                acc = psum.tile([P, width], F32, name="acc_y", tag="acc")
                nc.tensor.matmul_mx(out=acc[:], lhsT=w1_cd[t].bitcast(FP8X4), lhsT_scale=w1_sc[t],
                                    rhs=x_cd[:, c0 : c0 + width].bitcast(FP8X4), rhs_scale=x_sc[:, c0 : c0 + width], start=True, stop=True)
                if (t, k) != (0, 1):
                    nc.scalar.copy(out=y[t][:, c0 : c0 + width], in_=acc[:])
                else:
                    nc.vector.tensor_copy(out=y[t][:, c0 : c0 + width], in_=acc[:])

        def line_up(t, h):
            picked = y[t][:].indirect(order_sb[:, 32 * h : 32 * h + 32])
            dst = lined[t][:, HALF * h : HALF * (h + 1)]
            if (t, h) in ((0, 0), (1, 0), (1, 1)):
                nc.vector.tensor_scalar(dst, picked, 0.5, 0.0, ALU.mult, ALU.add)
            else:
                nc.scalar.activation(out=dst, in_=picked, func=ACT.Copy, scale=0.5)

        def pair_sum(eng, t, a, b):
            pr = lined[t][:, 2 * a : 2 * b].rearrange("p (v e) -> p v e", e=2)
            eng.tensor_tensor(out=means[t][:, a:b], in0=pr[:, :, 0], in1=pr[:, :, 1], op=ALU.add)

        for t in range(2):
            first_product(t)
        for h in range(2):
            line_up(0, h)
        for h in range(2):
            pair_sum(nc.gpsimd, 0, V // 2 * h, V // 2 * (h + 1))
        means[1] = keep.tile([P, V], F32, name="mean1", tag="lined0", align_bytes=64)
        for t in range(2, PACK):
            first_product(t)
        for t in range(1, PACK):
            for h in range(2):
                line_up(t, h)

        w2_g = keep.tile([P, N * PACK], BF16, name="w2_g", tag="lined1", align_bytes=64)
        nc.scalar.copy(out=w2_g[:].rearrange("p (c i t) -> p c t i", i=4, t=PACK), in_=w2_all[:].rearrange("p t (c i) -> p c t i", i=4))
        w2_cd = keep.tile([P, N], U32, name="w2_cd", align_bytes=64)
        w2_sc = keep.tile([P, N], U8, name="w2_sc", align_bytes=64)

        out_view = out.rearrange("(g p) s -> p g s", p=P)

        starts = [sum(CHUNKS[:ci]) for ci in range(len(CHUNKS))]
        places = (0, 2 * S, S, S - CHUNKS[0])
        diffs = [work[:, a : a + S].rearrange("p (t n) -> p t n", t=PACK) for a in places]
        joint = diffs.pop()
        diffs += [joint[:, :, : CHUNKS[3]], joint[:, :, CHUNKS[3] :]]
        cut = CHUNKS[2] - SHARE
        z_a = keep.tile([P, 2 * HALF + cut * PACK], BF16, name="z_a", align_bytes=64)
        z_b = keep.tile([P, 2 * HALF], BF16, name="z_b", align_bytes=64)
        zs = [z_a[:, cut * PACK :], z_b[:], z_a[:, : 2 * HALF], z_a[:, :HALF], z_a[:, HALF : 2 * HALF]]

        def front(ci, planes, both=False):
            c0, n = starts[ci], CHUNKS[0] if both else CHUNKS[ci]
            for t in planes:
                nc.vector.tensor_tensor((joint if both else diffs[ci])[:, t, :], means[t][:].indirect(bucket_sb[:, c0 // 16 : (c0 + n) // 16]), y[t][:, c0 : c0 + n], ALU.subtract)

        def relu(d, z, small):
            dst = z.rearrange("p (c i t) -> p c t i", i=4, t=PACK)
            src = d.rearrange("p t (c i) -> p c t i", i=4)
            if small:
                nc.vector.tensor_scalar(dst, src, -1.0, 0.0, ALU.mult, ALU.max)
            else:
                nc.scalar.activation(out=dst, in_=src, func=ACT.Relu, scale=-1.0)

        def product(n, z, per):
            z_cd = ring.tile([P, n], U32, name="z_cd", align_bytes=64)
            z_sc = ring.tile([P, n], U8, name="z_sc", align_bytes=64)
            nc.vector.quantize_mx(out=z_cd[:].bitcast(FP8X4), scales=z_sc[:], in_=z)
            banks = []
            for u in range(PACK // per):
                acc = psum.tile([P, per, n], F32, name="acc_o", tag="acc")
                for k in range(per):
                    g = per * u + k
                    nc.tensor.matmul_mx(out=acc[:, k, :], lhsT=w2_cd[:, P * g : P * (g + 1)].bitcast(FP8X4), lhsT_scale=w2_sc[:, P * g : P * (g + 1)],
                                        rhs=z_cd[:].bitcast(FP8X4), rhs_scale=z_sc[:], start=True, stop=True)
                banks.append(acc)
            return banks

        def leave(c0, n, banks, u, on_vector, queue):
            per = PACK // len(banks)
            res = keep.tile([P, per, n], F32, name=f"res{c0}_{u}", align_bytes=ROW_START)[:]
            if on_vector:
                nc.vector.tensor_copy(out=res, in_=banks[u][:])
            else:
                nc.scalar.copy(out=res, in_=banks[u][:])
            queue.dma_start(out=out_view[:, per * u : per * (u + 1), c0 : c0 + n], in_=res)

        def back(c0, n, z):
            banks = product(n, z, 2)
            for u in range(2):
                leave(c0, n, banks, u, False, nc.sync)

        front(0, [0])
        pair_sum(nc.vector, 1, 0, V)
        front(1, [0])
        front(0, [1])
        front(1, [1])
        front(2, [0])
        pair_sum(nc.vector, 2, 0, V)
        front(2, [1])
        front(0, [2])
        for h in range(2):
            pair_sum(nc.vector, 3, V // 2 * h, V // 2 * (h + 1))
        front(1, [2])
        front(0, [3])
        relu(diffs[0], zs[0], False)
        front(1, [3])
        relu(diffs[1], zs[1], False)
        front(2, [2])
        nc.vector.quantize_mx(out=w2_cd[:].bitcast(FP8X4), scales=w2_sc[:], in_=w2_g[:])
        front(2, [3])
        relu(diffs[2][:, :, :cut], zs[2][:, : cut * PACK], False)
        back(starts[0], CHUNKS[0], zs[0])
        front(3, [0], True)
        relu(diffs[2][:, :, cut:], zs[2][:, cut * PACK :], True)
        back(starts[1], CHUNKS[1], zs[1])
        front(3, [1], True)
        back(starts[2], CHUNKS[2], zs[2])
        front(3, [2], True)
        for ci in (3, 4):
            front(ci, [3])
        for ci in (3, 4):
            relu(diffs[ci], zs[ci], True)
        fourth = product(CHUNKS[3], zs[3], 2)
        fifth = product(CHUNKS[4], zs[4], 1)
        for u in range(2):
            leave(starts[3], CHUNKS[3], fourth, u, u == 1, nc.sync)
        for u in range(PACK):
            leave(starts[4], CHUNKS[4], fifth, u, u % 2 == 1, nc.scalar if u % 2 == 0 else nc.sync)
